import numpy as np
import ml_dtypes


def mxq(x, axis, fmt="e4m3"):
    dtype, down = {"e4m3": (ml_dtypes.float8_e4m3fn, 7), "e5m2": (ml_dtypes.float8_e5m2, 14)}[fmt]
    v = np.moveaxis(np.asarray(x, np.float32).astype(ml_dtypes.bfloat16).astype(np.float64), axis, -1)
    blocks = v.reshape(v.shape[:-1] + (-1, 32))
    amax = np.abs(blocks).max(-1, keepdims=True)
    byte = np.maximum(np.where(amax > 0, np.frexp(amax)[1] - 1 + 127, 0) - down, 1)
    scale = np.exp2(byte - 127.0)
    codes = (blocks / scale).astype(np.float32).astype(dtype).astype(np.float64)
    return np.moveaxis((codes * scale).reshape(v.shape), -1, axis)


WIDE = False


def mx_kscale(k):
    if not WIDE:
        return np.ones(k)
    levels = np.array([10, -10, 5, -5, 0])
    if k % 512:
        return np.exp2(np.random.permutation(np.resize(levels, k // 32))).repeat(32)
    a = np.empty((k // 512, 16))
    for p in range(k // 512):
        a[p, :8] = np.random.permutation(np.resize(levels, 8))
        for g in range(8):
            far = levels[np.abs(levels - a[p, g]) >= 10]
            a[p, g + 8] = far[np.random.randint(len(far))]
    return np.exp2(a.ravel()).repeat(32)


def f64(x):
    return np.asarray(x).astype(np.float64)


def striped(idx):
    return np.tile(idx.reshape(-1, 16).T, (8, 1)).astype(np.uint16)


def unstriped(offs):
    return offs[:16].T.reshape(-1).astype(np.int64)


E2M1 = np.array([0.0, 0.5, 1.0, 1.5, 2.0, 3.0, 4.0, 6.0, -0.0, -0.5, -1.0, -1.5, -2.0, -3.0, -4.0, -6.0])


def pack_fp4(w):
    k, n = w.shape
    w = f64(np.asarray(w, np.float32).astype(ml_dtypes.bfloat16)).reshape(k // 32, 32, n)
    amax = np.abs(w).max(1)
    mant, ex = np.frexp(amax / 6.0)
    byte = np.clip(np.where(amax > 0, np.where(mant > 0.5, ex, ex - 1) + 127, 1), 1, 254)
    scaled = (w * np.exp2(127.0 - byte)[:, None, :]).reshape(k, n).astype(np.float32)
    c = np.ascontiguousarray(scaled.reshape(k // 512, 128, 4, n).transpose(0, 1, 3, 2)).astype(ml_dtypes.float4_e2m1fn).view(np.uint8) & 0xF
    words = (c[..., 0::2] | (c[..., 1::2] << 4)).reshape(k // 512, 128, 2 * n)
    return np.ascontiguousarray(words), np.ascontiguousarray(byte.astype(np.uint8).reshape(k // 512, 16, n))


def unpack_fp4(words, scales):
    g, _, n = scales.shape
    words = np.ascontiguousarray(words).reshape(g, 128, n, 2)
    nib = np.empty((g, 128, n, 4), np.uint8)
    nib[..., 0::2] = words & 0xF
    nib[..., 1::2] = words >> 4
    vals = E2M1[nib] * np.repeat(np.exp2(scales.astype(np.float64) - 127.0), 8, axis=1)[..., None]
    return vals.transpose(0, 1, 3, 2).reshape(g * 512, n)


def sigmoid(v):
    return 1.0 / (1.0 + np.exp(-np.maximum(v, -700.0)))


def gelu(v):
    return 0.5 * v * (1.0 + np.tanh(np.sqrt(2.0 / np.pi) * (v + 0.044715 * v**3)))


K, T, S, N = 512, 2048, 1024, 256


def setup_inputs():
    n = np.random.standard_normal
    s = mx_kscale(K)[:, None]
    packed_xT = pack_fp4(n((K, T)) * s)
    return {
        "x_words": packed_xT[0],
        "x_scales": packed_xT[1],
        "res": n((N, T)).astype(np.float32),
        "w1": (n((K, N)) / np.sqrt(K) / s).astype(np.float32),
        "w2": (n((K, N)) / np.sqrt(K) / s).astype(np.float32),
        "offs": striped(np.random.permutation(T)[:S]),
    }


def reference(x_words, x_scales, res, w1, w2, offs):
    r = f64(res)[:, unstriped(offs)]
    xq = unpack_fp4(x_words, x_scales)[:, unstriped(offs)]
    g = sigmoid(mxq(f64(w2), 0, "e4m3").T @ xq)
    y = gelu(mxq(f64(w1), 0, "e4m3").T @ xq)
    return r + g * (y - r)

@@ -1,0 +1,140 @@
+from contextlib import ExitStack
+
+import concourse.mybir as mybir
+
+K, T, S, N = 512, 2048, 1024, 256
+FLOPS = 2 * 2 * K * N * S
+
+F32 = mybir.dt.float32
+BF16 = mybir.dt.bfloat16
+I32 = mybir.dt.int32
+U32 = mybir.dt.uint32
+U16 = mybir.dt.uint16
+U8 = mybir.dt.uint8
+FP8X4 = mybir.dt.float8_e4m3fn_x4
+FP4X4 = mybir.dt.float4_e2m1fn_x4
+ACT = mybir.ActivationFunctionType
+ALU = mybir.AluOpType
+
+P = 128
+PACK = 4
+CH = 512
+PER_COL = 16
+
+
+def tile_picked_highway_gelu_p_kernel(tc, x_words, x_scales, res, w1, w2, offs, out):
+    nc = tc.nc
+    with ExitStack() as ctx:
+        keep = ctx.enter_context(tc.tile_pool(name="keep", bufs=1))
+        psum = ctx.enter_context(tc.psum_pool(name="psum", bufs=1))
+
+        offsets = keep.tile([P, S // PER_COL], U16, name="offsets")
+        nc.sync.dma_start(offsets[:], offs)
+
+        scale_table = keep.tile([P, T], U8, name="scale_table", align_bytes=64)
+        nc.gpsimd.memset(scale_table[:].bitcast(I32), 0)
+        warm_in = keep.tile([P, 1], F32, name="warm_in")
+        nc.gpsimd.memset(warm_in[:], 0.0)
+        for q in range(4):
+            queue = nc.scalar if q < 2 else nc.gpsimd
+            queue.dma_start(
+                out=scale_table[32 * q : 32 * q + 4, :].bitcast(I32),
+                in_=x_scales[0, 4 * q : 4 * q + 4, :].bitcast(I32),
+            )
+
+        warm_out = keep.tile([P, 1], F32, name="warm_out")
+        nc.scalar.activation(warm_out[:], warm_in[:], ACT.Gelu_apprx_tanh)
+
+        raw = []
+        for i in range(2):
+            raw.append(keep.tile([P, PACK, N], F32, name=f"raw{i}"))
+        word_table = keep.tile([P, T], U16, name="word_table", align_bytes=64)
+        nc.sync.dma_start(out=word_table[:].bitcast(I32), in_=x_words[0].bitcast(I32))
+        nc.sync.dma_start(out=raw[0][:], in_=w1.rearrange("(p j) c -> p j c", j=PACK))
+        nc.sync.dma_start(out=raw[1][:], in_=w2.rearrange("(p j) c -> p j c", j=PACK))
+        res_rows = []
+        for m in range(N // P):
+            r = keep.tile([P, T], F32, name=f"res_rows{m}")
+            nc.sync.dma_start(out=r[:], in_=res[m * P : (m + 1) * P, :])
+            res_rows.append(r)
+
+        def entries(c):
+            return offsets[:, c * CH // PER_COL : (c + 1) * CH // PER_COL]
+
+        grouped = [keep.tile([P, N * PACK], BF16, name=f"grouped{i}", align_bytes=64) for i in range(2)]
+        codes = [keep.tile([P, N], U32, name=f"codes{i}", align_bytes=64) for i in range(2)]
+        scales = [keep.tile([P, N], U8, name=f"scales{i}", align_bytes=64) for i in range(2)]
+
+        def interleave(i):
+            nc.scalar.copy(
+                out=grouped[i][:].rearrange("p (c i t) -> p c t i", i=4, t=PACK),
+                in_=raw[i][:].rearrange("p t (c i) -> p c t i", i=4),
+            )
+
+        def quantize(i):
+            nc.vector.quantize_mx(out=codes[i][:].bitcast(FP8X4), scales=scales[i][:], in_=grouped[i][:])
+
+        picked_scales = [keep.tile([P, CH], U8, name=f"picked_scales{c}", align_bytes=64) for c in range(2)]
+        picked_words = [keep.tile([P, CH], U16, name=f"picked_words{c}", align_bytes=64) for c in range(2)]
+
+        interleave(0)
+        interleave(1)
+        for c in range(2):
+            nc.vector.tensor_copy(picked_words[c][:], word_table[:].indirect(entries(c)))
+        nc.vector.tensor_copy(picked_scales[0][:], scale_table[:].indirect(entries(0)))
+        quantize(0)
+        quantize(1)
+        nc.vector.tensor_copy(picked_scales[1][:], scale_table[:].indirect(entries(1)))
+
+        units = [(m, c) for m in range(N // P) for c in range(2)]
+        y, th, d, e, o = {}, {}, {}, {}, {}
+
+        def product(i, m, c):
+            acc = psum.tile([P, CH], F32, name=f"acc{i}{m}{c}")
+            nc.tensor.matmul_mx(
+                out=acc[:],
+                lhsT=codes[i][:, m * P : (m + 1) * P].bitcast(FP8X4),
+                lhsT_scale=scales[i][:, m * P : (m + 1) * P],
+                rhs=picked_words[c][:].bitcast(FP4X4),
+                rhs_scale=picked_scales[c][:],
+                start=True,
+                stop=True,
+            )
+            return acc
+
+        for u in units:
+            m, c = u
+            y[u] = keep.tile([P, CH], F32, name=f"y{m}{c}")
+            th[u] = keep.tile([P, CH], F32, name=f"th{m}{c}")
+            nc.scalar.activation(y[u][:], product(0, m, c)[:], ACT.Gelu_apprx_tanh)
+            nc.scalar.activation(th[u][:], product(1, m, c)[:], ACT.Tanh, scale=0.5)
+
+        def diff(u):
+            m, c = u
+            d[u] = keep.tile([P, CH], F32, name=f"d{m}{c}")
+            nc.vector.tensor_tensor(d[u][:], res_rows[m][:].indirect(entries(c)), y[u][:], ALU.subtract)
+
+        def gate(u):
+            m, c = u
+            e[u] = keep.tile([P, CH], F32, name=f"e{m}{c}")
+            nc.vector.scalar_tensor_tensor(e[u][:], th[u][:], 1.0, d[u][:], ALU.subtract, ALU.mult)
+
+        def finish(u):
+            m, c = u
+            o[u] = keep.tile([P, CH], F32, name=f"o{m}{c}")
+            nc.vector.scalar_tensor_tensor(o[u][:], e[u][:], -0.5, y[u][:], ALU.mult, ALU.add)
+            nc.sync.dma_start(out=out[m * P : (m + 1) * P, c * CH : (c + 1) * CH], in_=o[u][:])
+
+        u0, u1, u2, u3 = units
+        diff(u0)
+        diff(u1)
+        gate(u0)
+        diff(u2)
+        finish(u0)
+        gate(u1)
+        diff(u3)
+        finish(u1)
+        gate(u2)
+        gate(u3)
+        finish(u2)
+        finish(u3)

@@ -28,63 +28,68 @@ def tile_picked_highway_gelu_p_kernel(tc, x_words, x_scales, res, w1, w2, offs, 
         keep = ctx.enter_context(tc.tile_pool(name="keep", bufs=1))
         psum = ctx.enter_context(tc.psum_pool(name="psum", bufs=1))
 
+        word_table = keep.tile([P, T], U16, name="word_table", align_bytes=64)
+        nc.sync.dma_start(out=word_table[:].bitcast(I32), in_=x_words[0].bitcast(I32))
         offsets = keep.tile([P, S // PER_COL], U16, name="offsets")
         nc.sync.dma_start(offsets[:], offs)
 
         scale_table = keep.tile([P, T], U8, name="scale_table", align_bytes=64)
         nc.gpsimd.memset(scale_table[:].bitcast(I32), 0)
         warm_in = keep.tile([P, 1], F32, name="warm_in")
+        warm_out = keep.tile([P, 1], F32, name="warm_out")
         nc.gpsimd.memset(warm_in[:], 0.0)
+        nc.scalar.activation(warm_out[:], warm_in[:], ACT.Gelu_apprx_tanh)
         for q in range(4):
-            queue = nc.scalar if q < 2 else nc.gpsimd
-            queue.dma_start(
+            nc.sync.dma_start(
                 out=scale_table[32 * q : 32 * q + 4, :].bitcast(I32),
                 in_=x_scales[0, 4 * q : 4 * q + 4, :].bitcast(I32),
             )
 
-        warm_out = keep.tile([P, 1], F32, name="warm_out")
-        nc.scalar.activation(warm_out[:], warm_in[:], ACT.Gelu_apprx_tanh)
-
         raw = []
-        for i in range(2):
+        for i, w in enumerate((w1, w2)):
             raw.append(keep.tile([P, PACK, N], F32, name=f"raw{i}"))
-        word_table = keep.tile([P, T], U16, name="word_table", align_bytes=64)
-        nc.sync.dma_start(out=word_table[:].bitcast(I32), in_=x_words[0].bitcast(I32))
-        nc.sync.dma_start(out=raw[0][:], in_=w1.rearrange("(p j) c -> p j c", j=PACK))
-        nc.sync.dma_start(out=raw[1][:], in_=w2.rearrange("(p j) c -> p j c", j=PACK))
+            nc.sync.dma_start(out=raw[i][:], in_=w.rearrange("(p j) c -> p j c", j=PACK))
         res_rows = []
         for m in range(N // P):
             r = keep.tile([P, T], F32, name=f"res_rows{m}")
             nc.sync.dma_start(out=r[:], in_=res[m * P : (m + 1) * P, :])
             res_rows.append(r)
 
-        def entries(c):
-            return offsets[:, c * CH // PER_COL : (c + 1) * CH // PER_COL]
+        def entries(a, b):
+            return offsets[:, a // PER_COL : b // PER_COL]
 
-        grouped = [keep.tile([P, N * PACK], BF16, name=f"grouped{i}", align_bytes=64) for i in range(2)]
-        codes = [keep.tile([P, N], U32, name=f"codes{i}", align_bytes=64) for i in range(2)]
-        scales = [keep.tile([P, N], U8, name=f"scales{i}", align_bytes=64) for i in range(2)]
+        grouped, codes, scales = {}, {}, {}
+        for i in range(2):
+            for m in range(2):
+                grouped[i, m] = keep.tile([P, P * PACK], BF16, name=f"grouped{i}{m}", align_bytes=64)
+                codes[i, m] = keep.tile([P, P], U32, name=f"codes{i}{m}", align_bytes=64)
+                scales[i, m] = keep.tile([P, P], U8, name=f"scales{i}{m}", align_bytes=64)
+                nc.scalar.copy(
+                    out=grouped[i, m][:].rearrange("p (c i t) -> p c t i", i=4, t=PACK),
+                    in_=raw[i][:, :, m * P : (m + 1) * P].rearrange("p t (c i) -> p c t i", i=4),
+                )
 
-        def interleave(i):
-            nc.scalar.copy(
-                out=grouped[i][:].rearrange("p (c i t) -> p c t i", i=4, t=PACK),
-                in_=raw[i][:].rearrange("p t (c i) -> p c t i", i=4),
-            )
+        def quantize(i, m):
+            nc.vector.quantize_mx(out=codes[i, m][:].bitcast(FP8X4), scales=scales[i, m][:], in_=grouped[i, m][:])
 
-        def quantize(i):
-            nc.vector.quantize_mx(out=codes[i][:].bitcast(FP8X4), scales=scales[i][:], in_=grouped[i][:])
+        picked_words, picked_scales = {}, {}
 
-        picked_scales = [keep.tile([P, CH], U8, name=f"picked_scales{c}", align_bytes=64) for c in range(2)]
-        picked_words = [keep.tile([P, CH], U16, name=f"picked_words{c}", align_bytes=64) for c in range(2)]
+        def pick_words(c, tag):
+            picked_words[c] = keep.tile([P, CH], U16, name=f"picked_words{c}", tag=tag, align_bytes=64)
+            nc.vector.tensor_copy(picked_words[c][:], word_table[:].indirect(entries(c * CH, (c + 1) * CH)))
 
-        interleave(0)
-        interleave(1)
-        for c in range(2):
-            nc.vector.tensor_copy(picked_words[c][:], word_table[:].indirect(entries(c)))
-        nc.vector.tensor_copy(picked_scales[0][:], scale_table[:].indirect(entries(0)))
-        quantize(0)
-        quantize(1)
-        nc.vector.tensor_copy(picked_scales[1][:], scale_table[:].indirect(entries(1)))
+        def pick_scales(c, tag):
+            picked_scales[c] = keep.tile([P, CH], U8, name=f"picked_scales{c}", tag=tag, align_bytes=64)
+            nc.vector.tensor_copy(picked_scales[c][:], scale_table[:].indirect(entries(c * CH, (c + 1) * CH)))
+
+        pick_words(0, "picked_words0")
+        pick_scales(0, "picked_scales0")
+        quantize(0, 0)
+        pick_words(1, "grouped00")
+        quantize(0, 1)
+        quantize(1, 0)
+        quantize(1, 1)
+        pick_scales(1, "grouped11")
 
         units = [(m, c) for m in range(N // P) for c in range(2)]
         y, th, d, e, o = {}, {}, {}, {}, {}
@@ -93,8 +98,8 @@ def tile_picked_highway_gelu_p_kernel(tc, x_words, x_scales, res, w1, w2, offs, 
             acc = psum.tile([P, CH], F32, name=f"acc{i}{m}{c}")
             nc.tensor.matmul_mx(
                 out=acc[:],
-                lhsT=codes[i][:, m * P : (m + 1) * P].bitcast(FP8X4),
-                lhsT_scale=scales[i][:, m * P : (m + 1) * P],
+                lhsT=codes[i, m][:].bitcast(FP8X4),
+                lhsT_scale=scales[i, m][:],
                 rhs=picked_words[c][:].bitcast(FP4X4),
                 rhs_scale=picked_scales[c][:],
                 start=True,
@@ -107,34 +112,35 @@ def tile_picked_highway_gelu_p_kernel(tc, x_words, x_scales, res, w1, w2, offs, 
             y[u] = keep.tile([P, CH], F32, name=f"y{m}{c}")
             th[u] = keep.tile([P, CH], F32, name=f"th{m}{c}")
             nc.scalar.activation(y[u][:], product(0, m, c)[:], ACT.Gelu_apprx_tanh)
-            nc.scalar.activation(th[u][:], product(1, m, c)[:], ACT.Tanh, scale=0.5)
+            nc.scalar.activation(th[u][:], product(1, m, c)[:], ACT.Tanh, scale=-0.5)
 
         def diff(u):
             m, c = u
             d[u] = keep.tile([P, CH], F32, name=f"d{m}{c}")
-            nc.vector.tensor_tensor(d[u][:], res_rows[m][:].indirect(entries(c)), y[u][:], ALU.subtract)
+            nc.vector.tensor_tensor(d[u][:], res_rows[m][:].indirect(entries(c * CH, (c + 1) * CH)), y[u][:], ALU.subtract)
 
         def gate(u):
             m, c = u
             e[u] = keep.tile([P, CH], F32, name=f"e{m}{c}")
-            nc.vector.scalar_tensor_tensor(e[u][:], th[u][:], 1.0, d[u][:], ALU.subtract, ALU.mult)
+            nc.vector.scalar_tensor_tensor(e[u][:], th[u][:], 1.0, d[u][:], ALU.add, ALU.mult)
 
-        def finish(u):
+        def finish(u, a, b):
             m, c = u
-            o[u] = keep.tile([P, CH], F32, name=f"o{m}{c}")
-            nc.vector.scalar_tensor_tensor(o[u][:], e[u][:], -0.5, y[u][:], ALU.mult, ALU.add)
-            nc.sync.dma_start(out=out[m * P : (m + 1) * P, c * CH : (c + 1) * CH], in_=o[u][:])
+            piece = keep.tile([P, b - a], F32, name=f"o{m}{c}{a}")
+            nc.vector.scalar_tensor_tensor(piece[:], e[u][:, a:b], 0.5, y[u][:, a:b], ALU.mult, ALU.add)
+            nc.sync.dma_start(out=out[m * P : (m + 1) * P, c * CH + a : c * CH + b], in_=piece[:])
 
         u0, u1, u2, u3 = units
         diff(u0)
         diff(u1)
         gate(u0)
         diff(u2)
-        finish(u0)
+        finish(u0, 0, CH)
         gate(u1)
         diff(u3)
-        finish(u1)
+        finish(u1, 0, CH)
         gate(u2)
         gate(u3)
-        finish(u2)
-        finish(u3)
+        finish(u2, 0, CH)
+        finish(u3, 0, 384)
+        finish(u3, 384, CH)

@@ -1,6 +1,7 @@
 from contextlib import ExitStack
 
 import concourse.mybir as mybir
+from concourse.masks import make_identity
 
 K, T, S, N = 512, 2048, 1024, 256
 FLOPS = 2 * 2 * K * N * S
@@ -20,13 +21,14 @@ P = 128
 PACK = 4
 CH = 512
 PER_COL = 16
+BLOCKS = CH // P
 
 
 def tile_picked_highway_gelu_p_kernel(tc, x_words, x_scales, res, w1, w2, offs, out):
     nc = tc.nc
     with ExitStack() as ctx:
         keep = ctx.enter_context(tc.tile_pool(name="keep", bufs=1))
-        psum = ctx.enter_context(tc.psum_pool(name="psum", bufs=1))
+        products = ctx.enter_context(tc.psum_pool(name="products", bufs=1))
 
         word_table = keep.tile([P, T], U16, name="word_table", align_bytes=64)
         nc.sync.dma_start(out=word_table[:].bitcast(I32), in_=x_words[0].bitcast(I32))
@@ -44,6 +46,8 @@ def tile_picked_highway_gelu_p_kernel(tc, x_words, x_scales, res, w1, w2, offs, 
                 out=scale_table[32 * q : 32 * q + 4, :].bitcast(I32),
                 in_=x_scales[0, 4 * q : 4 * q + 4, :].bitcast(I32),
             )
+        identity = keep.tile([P, P], F32, name="identity")
+        make_identity(nc, identity[:])
 
         raw = []
         for i, w in enumerate((w1, w2)):
@@ -55,51 +59,51 @@ def tile_picked_highway_gelu_p_kernel(tc, x_words, x_scales, res, w1, w2, offs, 
             nc.sync.dma_start(out=r[:], in_=res[m * P : (m + 1) * P, :])
             res_rows.append(r)
 
-        def entries(a, b):
-            return offsets[:, a // PER_COL : b // PER_COL]
+        def entries(c):
+            return offsets[:, c * CH // PER_COL : (c + 1) * CH // PER_COL]
 
         grouped, codes, scales = {}, {}, {}
         for i in range(2):
-            for m in range(2):
-                grouped[i, m] = keep.tile([P, P * PACK], BF16, name=f"grouped{i}{m}", align_bytes=64)
-                codes[i, m] = keep.tile([P, P], U32, name=f"codes{i}{m}", align_bytes=64)
-                scales[i, m] = keep.tile([P, P], U8, name=f"scales{i}{m}", align_bytes=64)
-                nc.scalar.copy(
-                    out=grouped[i, m][:].rearrange("p (c i t) -> p c t i", i=4, t=PACK),
-                    in_=raw[i][:, :, m * P : (m + 1) * P].rearrange("p t (c i) -> p c t i", i=4),
-                )
+            grouped[i] = keep.tile([P, N * PACK], BF16, name=f"grouped{i}", align_bytes=64)
+            codes[i] = keep.tile([P, N], U32, name=f"codes{i}", align_bytes=64)
+            scales[i] = keep.tile([P, N], U8, name=f"scales{i}", align_bytes=64)
+            nc.scalar.copy(
+                out=grouped[i][:].rearrange("p (c i t) -> p c t i", i=4, t=PACK),
+                in_=raw[i][:].rearrange("p t (c i) -> p c t i", i=4),
+            )
 
-        def quantize(i, m):
-            nc.vector.quantize_mx(out=codes[i, m][:].bitcast(FP8X4), scales=scales[i, m][:], in_=grouped[i, m][:])
+        def quantize(i):
+            nc.vector.quantize_mx(out=codes[i][:].bitcast(FP8X4), scales=scales[i][:], in_=grouped[i][:])
 
         picked_words, picked_scales = {}, {}
 
-        def pick_words(c, tag):
-            picked_words[c] = keep.tile([P, CH], U16, name=f"picked_words{c}", tag=tag, align_bytes=64)
-            nc.vector.tensor_copy(picked_words[c][:], word_table[:].indirect(entries(c * CH, (c + 1) * CH)))
+        def pick_words(c):
+            picked_words[c] = keep.tile([P, CH], U16, name=f"picked_words{c}", align_bytes=64)
+            nc.vector.tensor_copy(picked_words[c][:], word_table[:].indirect(entries(c)))
 
         def pick_scales(c, tag):
             picked_scales[c] = keep.tile([P, CH], U8, name=f"picked_scales{c}", tag=tag, align_bytes=64)
-            nc.vector.tensor_copy(picked_scales[c][:], scale_table[:].indirect(entries(c * CH, (c + 1) * CH)))
+            nc.vector.tensor_copy(picked_scales[c][:], scale_table[:].indirect(entries(c)))
 
-        pick_words(0, "picked_words0")
+        pick_words(0)
+        pick_words(1)
         pick_scales(0, "picked_scales0")
-        quantize(0, 0)
-        pick_words(1, "grouped00")
-        quantize(0, 1)
-        quantize(1, 0)
-        quantize(1, 1)
-        pick_scales(1, "grouped11")
+        quantize(0)
+        pick_scales(1, "grouped0")
+        quantize(1)
 
-        units = [(m, c) for m in range(N // P) for c in range(2)]
-        y, th, d, e, o = {}, {}, {}, {}, {}
+        y, th, d, e, y2, total = {}, {}, {}, {}, {}, {}
 
-        def product(i, m, c):
-            acc = psum.tile([P, CH], F32, name=f"acc{i}{m}{c}")
+        def block(b):
+            return slice(b * P, (b + 1) * P)
+
+        def product(i, u):
+            m, c = u
+            acc = products.tile([P, CH], F32, name="acc", tag=f"bank{i}{c}")
             nc.tensor.matmul_mx(
                 out=acc[:],
-                lhsT=codes[i, m][:].bitcast(FP8X4),
-                lhsT_scale=scales[i, m][:],
+                lhsT=codes[i][:, block(m)].bitcast(FP8X4),
+                lhsT_scale=scales[i][:, block(m)],
                 rhs=picked_words[c][:].bitcast(FP4X4),
                 rhs_scale=picked_scales[c][:],
                 start=True,
@@ -107,40 +111,102 @@ def tile_picked_highway_gelu_p_kernel(tc, x_words, x_scales, res, w1, w2, offs, 
             )
             return acc
 
-        for u in units:
+        def product_turned(i, u):
             m, c = u
-            y[u] = keep.tile([P, CH], F32, name=f"y{m}{c}")
-            th[u] = keep.tile([P, CH], F32, name=f"th{m}{c}")
-            nc.scalar.activation(y[u][:], product(0, m, c)[:], ACT.Gelu_apprx_tanh)
-            nc.scalar.activation(th[u][:], product(1, m, c)[:], ACT.Tanh, scale=-0.5)
+            acc = products.tile([P, CH], F32, name="acc", tag=f"bank{i}{c}")
+            for b in range(BLOCKS):
+                nc.tensor.matmul_mx(
+                    out=acc[:, block(b)],
+                    lhsT=picked_words[c][:, block(b)].bitcast(FP4X4),
+                    lhsT_scale=picked_scales[c][:, block(b)],
+                    rhs=codes[i][:, block(m)].bitcast(FP8X4),
+                    rhs_scale=scales[i][:, block(m)],
+                    start=True,
+                    stop=True,
+                )
+            return acc
+
+        def sbuf(kind, u):
+            return keep.tile([P, CH], F32, name=f"{kind}{u[0]}{u[1]}")
+
+        def layer(u):
+            y[u] = sbuf("y", u)
+            nc.scalar.activation(y[u][:], product(0, u)[:], ACT.Gelu_apprx_tanh)
+
+        def gate_tanh(u, turned):
+            th[u] = sbuf("th", u)
+            acc = product_turned(1, u) if turned else product(1, u)
+            nc.scalar.activation(th[u][:], acc[:], ACT.Tanh, scale=-0.5)
+
+        def turn(src, i, u):
+            bank = products.tile([P, CH], F32, name="turned", tag=f"turn{i}{u[1]}")
+            for b in range(BLOCKS):
+                nc.tensor.transpose(bank[:, block(b)], src[:, block(b)], identity[:])
+            return bank
+
+        def turn_y(u):
+            y2[u] = sbuf("y2", u)
+            nc.scalar.activation(y2[u][:], turn(y[u], 0, u)[:], ACT.Copy, scale=2.0)
+
+        def open_sum(u):
+            total[u] = products.tile([P, CH], F32, name="total", tag=f"turn0{u[1]}")
+            for b in range(BLOCKS):
+                nc.tensor.matmul(
+                    total[u][:, block(b)], y2[u][:, block(b)], identity[:], start=(b == 0), stop=False, is_transpose=True
+                )
 
         def diff(u):
             m, c = u
-            d[u] = keep.tile([P, CH], F32, name=f"d{m}{c}")
-            nc.vector.tensor_tensor(d[u][:], res_rows[m][:].indirect(entries(c * CH, (c + 1) * CH)), y[u][:], ALU.subtract)
+            d[u] = sbuf("d", u)
+            nc.vector.tensor_tensor(d[u][:], res_rows[m][:].indirect(entries(c)), y[u][:], ALU.subtract)
 
-        def gate(u):
+        def gate(u, turned, tag=None):
+            e[u] = keep.tile([P, CH], F32, name=f"e{u[0]}{u[1]}", tag=tag or f"e{u[0]}{u[1]}")
+            src = turn(d[u], 1, u) if turned else d[u]
+            nc.vector.scalar_tensor_tensor(e[u][:], th[u][:], 1.0, src[:], ALU.add, ALU.mult)
+
+        def store(u, a, b, piece, queue):
             m, c = u
-            e[u] = keep.tile([P, CH], F32, name=f"e{m}{c}")
-            nc.vector.scalar_tensor_tensor(e[u][:], th[u][:], 1.0, d[u][:], ALU.add, ALU.mult)
+            queue.dma_start(out=out[block(m), c * CH + a : c * CH + b], in_=piece[:])
+
+        def close_sum(u):
+            for b in range(BLOCKS):
+                nc.tensor.matmul(
+                    total[u][:, block(b)], e[u][:, block(b)], identity[:], start=False, stop=(b == BLOCKS - 1), is_transpose=True
+                )
+            piece = sbuf("o", u)
+            nc.scalar.activation(piece[:], total[u][:], ACT.Copy, scale=0.5)
+            store(u, 0, CH, piece, nc.scalar)
 
         def finish(u, a, b):
             m, c = u
             piece = keep.tile([P, b - a], F32, name=f"o{m}{c}{a}")
             nc.vector.scalar_tensor_tensor(piece[:], e[u][:, a:b], 0.5, y[u][:, a:b], ALU.mult, ALU.add)
-            nc.sync.dma_start(out=out[m * P : (m + 1) * P, c * CH + a : c * CH + b], in_=piece[:])
+            store(u, a, b, piece, nc.sync)
 
-        u0, u1, u2, u3 = units
+        u0, u1, u2, u3 = (0, 0), (0, 1), (1, 0), (1, 1)
+        layer(u0)
+        layer(u1)
         diff(u0)
+        gate_tanh(u0, True)
         diff(u1)
-        gate(u0)
+        layer(u2)
+        gate_tanh(u1, True)
+        gate(u0, True)
+        gate(u1, True)
+        layer(u3)
+        turn_y(u0)
         diff(u2)
-        finish(u0, 0, CH)
-        gate(u1)
+        turn_y(u1)
+        open_sum(u0)
+        close_sum(u0)
+        gate_tanh(u2, False)
         diff(u3)
-        finish(u1, 0, CH)
-        gate(u2)
-        gate(u3)
+        gate_tanh(u3, False)
+        open_sum(u1)
+        close_sum(u1)
+        gate(u2, False)
+        gate(u3, False)
         finish(u2, 0, CH)
         finish(u3, 0, 384)
         finish(u3, 384, CH)

@@ -49,9 +49,9 @@ def tile_picked_highway_gelu_p_kernel(tc, x_words, x_scales, res, w1, w2, offs, 
         identity = keep.tile([P, P], F32, name="identity")
         make_identity(nc, identity[:])
 
-        raw = []
-        for i, w in enumerate((w1, w2)):
-            raw.append(keep.tile([P, PACK, N], F32, name=f"raw{i}"))
+        raw = {}
+        for i, w in ((1, w2), (0, w1)):
+            raw[i] = keep.tile([P, PACK, N], F32, name=f"raw{i}", align_bytes=64)
             nc.sync.dma_start(out=raw[i][:], in_=w.rearrange("(p j) c -> p j c", j=PACK))
         res_rows = []
         for m in range(N // P):
@@ -63,7 +63,7 @@ def tile_picked_highway_gelu_p_kernel(tc, x_words, x_scales, res, w1, w2, offs, 
             return offsets[:, c * CH // PER_COL : (c + 1) * CH // PER_COL]
 
         grouped, codes, scales = {}, {}, {}
-        for i in range(2):
+        for i in (1, 0):
             grouped[i] = keep.tile([P, N * PACK], BF16, name=f"grouped{i}", align_bytes=64)
             codes[i] = keep.tile([P, N], U32, name=f"codes{i}", align_bytes=64)
             scales[i] = keep.tile([P, N], U8, name=f"scales{i}", align_bytes=64)
@@ -88,18 +88,18 @@ def tile_picked_highway_gelu_p_kernel(tc, x_words, x_scales, res, w1, w2, offs, 
         pick_words(0)
         pick_words(1)
         pick_scales(0, "picked_scales0")
-        quantize(0)
-        pick_scales(1, "grouped0")
         quantize(1)
+        quantize(0)
+        pick_scales(1, "raw0")
 
-        y, th, d, e, y2, total = {}, {}, {}, {}, {}, {}
+        y, th, rest, mixed, picked, kept, total, d, e = {}, {}, {}, {}, {}, {}, {}, {}, {}
 
         def block(b):
             return slice(b * P, (b + 1) * P)
 
         def product(i, u):
             m, c = u
-            acc = products.tile([P, CH], F32, name="acc", tag=f"bank{i}{c}")
+            acc = products.tile([P, CH], F32, name="acc", tag=f"bank{i}00")
             nc.tensor.matmul_mx(
                 out=acc[:],
                 lhsT=codes[i][:, block(m)].bitcast(FP8X4),
@@ -113,7 +113,7 @@ def tile_picked_highway_gelu_p_kernel(tc, x_words, x_scales, res, w1, w2, offs, 
 
         def product_turned(i, u):
             m, c = u
-            acc = products.tile([P, CH], F32, name="acc", tag=f"bank{i}{c}")
+            acc = products.tile([P, CH], F32, name="acc", tag=f"bank{i}{m}{c}")
             for b in range(BLOCKS):
                 nc.tensor.matmul_mx(
                     out=acc[:, block(b)],
@@ -131,82 +131,108 @@ def tile_picked_highway_gelu_p_kernel(tc, x_words, x_scales, res, w1, w2, offs, 
 
         def layer(u):
             y[u] = sbuf("y", u)
-            nc.scalar.activation(y[u][:], product(0, u)[:], ACT.Gelu_apprx_tanh)
+            nc.scalar.activation(y[u][:], z[0, u][:], ACT.Gelu_apprx_tanh)
 
-        def gate_tanh(u, turned):
+        def gate_tanh(u):
             th[u] = sbuf("th", u)
-            acc = product_turned(1, u) if turned else product(1, u)
-            nc.scalar.activation(th[u][:], acc[:], ACT.Tanh, scale=-0.5)
+            nc.scalar.activation(th[u][:], z[1, u][:], ACT.Tanh, scale=-0.5)
 
-        def turn(src, i, u):
-            bank = products.tile([P, CH], F32, name="turned", tag=f"turn{i}{u[1]}")
+        def complement(u):
+            rest[u] = sbuf("rest", u)
+            nc.gpsimd.tensor_scalar(rest[u][:], th[u][:], -1.0, 1.0, ALU.mult, ALU.add)
+
+        def complement_scalar(u):
+            rest[u] = sbuf("rest", u)
+            nc.scalar.activation(rest[u][:], th[u][:], ACT.Identity, bias=1.0, scale=-1.0)
+
+        def mix(u):
+            mixed[u] = sbuf("mixed", u)
+            nc.gpsimd.tensor_tensor(mixed[u][:], rest[u][:], y[u][:], ALU.mult)
+
+        def pick_res(u, width):
+            m, c = u
+            picked[u] = sbuf("picked", u)
+            for a in range(0, CH, width):
+                part = offsets[:, (c * CH + a) // PER_COL : (c * CH + a + width) // PER_COL]
+                nc.vector.tensor_copy(picked[u][:, a : a + width], res_rows[m][:].indirect(part))
+
+        def keep_res(u, tag):
+            bank = products.tile([P, CH], F32, name="turned", tag=tag)
             for b in range(BLOCKS):
-                nc.tensor.transpose(bank[:, block(b)], src[:, block(b)], identity[:])
-            return bank
+                nc.tensor.transpose(bank[:, block(b)], picked[u][:, block(b)], identity[:])
+            kept[u] = sbuf("kept", u)
+            nc.vector.scalar_tensor_tensor(kept[u][:], th[u][:], 1.0, bank[:], ALU.add, ALU.mult)
 
-        def turn_y(u):
-            y2[u] = sbuf("y2", u)
-            nc.scalar.activation(y2[u][:], turn(y[u], 0, u)[:], ACT.Copy, scale=2.0)
-
-        def open_sum(u):
-            total[u] = products.tile([P, CH], F32, name="total", tag=f"turn0{u[1]}")
+        def open_sum(u, tag, first):
+            total[u] = products.tile([P, CH], F32, name="total", tag=tag)
             for b in range(BLOCKS):
                 nc.tensor.matmul(
-                    total[u][:, block(b)], y2[u][:, block(b)], identity[:], start=(b == 0), stop=False, is_transpose=True
+                    total[u][:, block(b)], first[u][:, block(b)], identity[:], start=(b == 0), stop=False, is_transpose=True
                 )
-
-        def diff(u):
-            m, c = u
-            d[u] = sbuf("d", u)
-            nc.vector.tensor_tensor(d[u][:], res_rows[m][:].indirect(entries(c)), y[u][:], ALU.subtract)
-
-        def gate(u, turned, tag=None):
-            e[u] = keep.tile([P, CH], F32, name=f"e{u[0]}{u[1]}", tag=tag or f"e{u[0]}{u[1]}")
-            src = turn(d[u], 1, u) if turned else d[u]
-            nc.vector.scalar_tensor_tensor(e[u][:], th[u][:], 1.0, src[:], ALU.add, ALU.mult)
 
         def store(u, a, b, piece, queue):
             m, c = u
             queue.dma_start(out=out[block(m), c * CH + a : c * CH + b], in_=piece[:])
 
-        def close_sum(u):
+        def close_sum(u, last):
             for b in range(BLOCKS):
                 nc.tensor.matmul(
-                    total[u][:, block(b)], e[u][:, block(b)], identity[:], start=False, stop=(b == BLOCKS - 1), is_transpose=True
+                    total[u][:, block(b)], last[u][:, block(b)], identity[:], start=False, stop=(b == BLOCKS - 1), is_transpose=True
                 )
             piece = sbuf("o", u)
             nc.scalar.activation(piece[:], total[u][:], ACT.Copy, scale=0.5)
             store(u, 0, CH, piece, nc.scalar)
 
+        def diff(u, a, b, tag):
+            m, c = u
+            d[u, a] = keep.tile([P, b - a], F32, name=f"d{m}{c}{a}", tag=tag)
+            part = offsets[:, (c * CH + a) // PER_COL : (c * CH + b) // PER_COL]
+            nc.vector.tensor_tensor(d[u, a][:], res_rows[m][:].indirect(part), y[u][:, a:b], ALU.subtract)
+
+        def gate(u, a, b, tag):
+            m, c = u
+            e[u, a] = keep.tile([P, b - a], F32, name=f"e{m}{c}{a}", tag=tag)
+            nc.vector.scalar_tensor_tensor(e[u, a][:], th[u][:, a:b], 1.0, d[u, a][:], ALU.add, ALU.mult)
+
         def finish(u, a, b):
             m, c = u
             piece = keep.tile([P, b - a], F32, name=f"o{m}{c}{a}")
-            nc.vector.scalar_tensor_tensor(piece[:], e[u][:, a:b], 0.5, y[u][:, a:b], ALU.mult, ALU.add)
+            nc.vector.scalar_tensor_tensor(piece[:], e[u, a][:], 0.5, y[u][:, a:b], ALU.mult, ALU.add)
             store(u, a, b, piece, nc.sync)
 
         u0, u1, u2, u3 = (0, 0), (0, 1), (1, 0), (1, 1)
-        layer(u0)
+        z = {}
+        for u in (u0, u2, u1):
+            for i in (1, 0):
+                z[i, u] = product_turned(i, u)
+        for i in (0, 1):
+            z[i, u3] = product(i, u3)
+        for u in (u0, u2):
+            gate_tanh(u)
+            layer(u)
+            complement(u)
+            mix(u)
+        gate_tanh(u1)
+        complement_scalar(u1)
         layer(u1)
-        diff(u0)
-        gate_tanh(u0, True)
-        diff(u1)
-        layer(u2)
-        gate_tanh(u1, True)
-        gate(u0, True)
-        gate(u1, True)
+        mix(u1)
         layer(u3)
-        turn_y(u0)
-        diff(u2)
-        turn_y(u1)
-        open_sum(u0)
-        close_sum(u0)
-        gate_tanh(u2, False)
-        diff(u3)
-        gate_tanh(u3, False)
-        open_sum(u1)
-        close_sum(u1)
-        gate(u2, False)
-        gate(u3, False)
-        finish(u2, 0, CH)
+        gate_tanh(u3)
+        pick_res(u0, CH)
+        pick_res(u1, 256)
+        keep_res(u0, "turn0")
+        keep_res(u1, "turn1")
+        pick_res(u2, CH)
+        diff(u3, 0, 384, "d110")
+        keep_res(u2, "bank101")
+        diff(u3, 384, CH, "picked10")
+        open_sum(u0, "bank110", mixed)
+        close_sum(u0, kept)
+        open_sum(u2, "bank010", mixed)
+        open_sum(u1, "bank001", kept)
+        close_sum(u1, mixed)
+        close_sum(u2, kept)
+        gate(u3, 0, 384, "th10")
+        gate(u3, 384, CH, "e11")
         finish(u3, 0, 384)
         finish(u3, 384, CH)

@@ -77,18 +77,18 @@ def tile_picked_highway_gelu_p_kernel(tc, x_words, x_scales, res, w1, w2, offs, 
 
         picked_words, picked_scales = {}, {}
 
-        def pick_words(c):
-            picked_words[c] = keep.tile([P, CH], U16, name=f"picked_words{c}", align_bytes=64)
+        def pick_words(c, tag):
+            picked_words[c] = keep.tile([P, CH], U16, name=f"picked_words{c}", tag=tag, align_bytes=64)
             nc.vector.tensor_copy(picked_words[c][:], word_table[:].indirect(entries(c)))
 
         def pick_scales(c, tag):
             picked_scales[c] = keep.tile([P, CH], U8, name=f"picked_scales{c}", tag=tag, align_bytes=64)
             nc.vector.tensor_copy(picked_scales[c][:], scale_table[:].indirect(entries(c)))
 
-        pick_words(0)
-        pick_words(1)
+        pick_words(0, "picked_words0")
         pick_scales(0, "picked_scales0")
         quantize(1)
+        pick_words(1, "raw1")
         quantize(0)
         pick_scales(1, "raw0")
 
@@ -145,43 +145,47 @@ def tile_picked_highway_gelu_p_kernel(tc, x_words, x_scales, res, w1, w2, offs, 
             rest[u] = sbuf("rest", u)
             nc.scalar.activation(rest[u][:], th[u][:], ACT.Identity, bias=1.0, scale=-1.0)
 
-        def mix(u):
-            mixed[u] = sbuf("mixed", u)
+        def mix(u, tag):
+            mixed[u] = keep.tile([P, CH], F32, name=f"mixed{u[0]}{u[1]}", tag=tag)
             nc.gpsimd.tensor_tensor(mixed[u][:], rest[u][:], y[u][:], ALU.mult)
 
-        def pick_res(u, width):
+        def pick_res(u, a, b, tag=None):
             m, c = u
-            picked[u] = sbuf("picked", u)
-            for a in range(0, CH, width):
-                part = offsets[:, (c * CH + a) // PER_COL : (c * CH + a + width) // PER_COL]
-                nc.vector.tensor_copy(picked[u][:, a : a + width], res_rows[m][:].indirect(part))
+            picked[u, a] = keep.tile([P, b - a], F32, name=f"picked{m}{c}{a}", tag=tag or f"picked{m}{c}{a}")
+            part = offsets[:, (c * CH + a) // PER_COL : (c * CH + b) // PER_COL]
+            nc.vector.tensor_copy(picked[u, a][:], res_rows[m][:].indirect(part))
 
-        def keep_res(u, tag):
-            bank = products.tile([P, CH], F32, name="turned", tag=tag)
-            for b in range(BLOCKS):
-                nc.tensor.transpose(bank[:, block(b)], picked[u][:, block(b)], identity[:])
-            kept[u] = sbuf("kept", u)
-            nc.vector.scalar_tensor_tensor(kept[u][:], th[u][:], 1.0, bank[:], ALU.add, ALU.mult)
+        def turn_res(u, a, b, bank, at):
+            for k in range((b - a) // P):
+                nc.tensor.transpose(bank[:, at + k * P : at + (k + 1) * P], picked[u, a][:, block(k)], identity[:])
 
-        def open_sum(u, tag, first):
-            total[u] = products.tile([P, CH], F32, name="total", tag=tag)
-            for b in range(BLOCKS):
+        def new_bank(tag):
+            return products.tile([P, CH], F32, name="bank", tag=tag)
+
+        def keep_res(u, a, b, bank):
+            nc.vector.scalar_tensor_tensor(kept[u][:, a:b], th[u][:, a:b], 1.0, bank[:, 0 : b - a], ALU.add, ALU.mult)
+
+        def add_turned(bank, src, a, b, first):
+            n = (b - a) // P
+            for k in range(n):
                 nc.tensor.matmul(
-                    total[u][:, block(b)], first[u][:, block(b)], identity[:], start=(b == 0), stop=False, is_transpose=True
+                    bank[:, block(k)],
+                    src[:, a + k * P : a + (k + 1) * P],
+                    identity[:],
+                    start=(first and k == 0),
+                    stop=(not first and k == n - 1),
+                    is_transpose=True,
                 )
 
         def store(u, a, b, piece, queue):
             m, c = u
             queue.dma_start(out=out[block(m), c * CH + a : c * CH + b], in_=piece[:])
 
-        def close_sum(u, last):
-            for b in range(BLOCKS):
-                nc.tensor.matmul(
-                    total[u][:, block(b)], last[u][:, block(b)], identity[:], start=False, stop=(b == BLOCKS - 1), is_transpose=True
-                )
-            piece = sbuf("o", u)
-            nc.scalar.activation(piece[:], total[u][:], ACT.Copy, scale=0.5)
-            store(u, 0, CH, piece, nc.scalar)
+        def empty(u, a, b, bank):
+            m, c = u
+            piece = keep.tile([P, b - a], F32, name=f"o{m}{c}{a}")
+            nc.scalar.activation(piece[:], bank[:, 0 : b - a], ACT.Copy, scale=0.5)
+            store(u, a, b, piece, nc.scalar)
 
         def diff(u, a, b, tag):
             m, c = u
@@ -202,37 +206,53 @@ def tile_picked_highway_gelu_p_kernel(tc, x_words, x_scales, res, w1, w2, offs, 
 
         u0, u1, u2, u3 = (0, 0), (0, 1), (1, 0), (1, 1)
         z = {}
-        for u in (u0, u2, u1):
-            for i in (1, 0):
-                z[i, u] = product_turned(i, u)
+        for i, u in ((1, u0), (1, u2), (0, u0), (0, u2), (1, u1), (0, u1)):
+            z[i, u] = product_turned(i, u)
         for i in (0, 1):
             z[i, u3] = product(i, u3)
-        for u in (u0, u2):
+        for u in (u0, u2, u1):
             gate_tanh(u)
+            complement_scalar(u)
             layer(u)
-            complement(u)
-            mix(u)
-        gate_tanh(u1)
-        complement_scalar(u1)
-        layer(u1)
-        mix(u1)
+            mix(u, f"mixed{u[0]}{u[1]}")
         layer(u3)
+        H = CH // 2
+        for u in (u0, u1, u2):
+            kept[u] = sbuf("kept", u)
+        pick_res(u0, 0, CH)
+        pick_res(u1, 0, H)
+        pick_res(u1, H, CH)
+        t0 = new_bank("turn0")
+        turn_res(u0, 0, CH, t0, 0)
+        keep_res(u0, 0, CH, t0)
+        t1 = new_bank("turn1")
+        turn_res(u1, 0, H, t1, 0)
+        turn_res(u1, H, CH, t1, H)
+        keep_res(u1, 0, CH, t1)
+        s0 = new_bank("bank110")
+        add_turned(s0, mixed[u0], 0, CH, True)
+        add_turned(s0, kept[u0], 0, CH, False)
+        empty(u0, 0, CH, s0)
+        s1 = new_bank("bank001")
         gate_tanh(u3)
-        pick_res(u0, CH)
-        pick_res(u1, 256)
-        keep_res(u0, "turn0")
-        keep_res(u1, "turn1")
-        pick_res(u2, CH)
-        diff(u3, 0, 384, "d110")
-        keep_res(u2, "bank101")
-        diff(u3, 384, CH, "picked10")
-        open_sum(u0, "bank110", mixed)
-        close_sum(u0, kept)
-        open_sum(u2, "bank010", mixed)
-        open_sum(u1, "bank001", kept)
-        close_sum(u1, mixed)
-        close_sum(u2, kept)
-        gate(u3, 0, 384, "th10")
-        gate(u3, 384, CH, "e11")
-        finish(u3, 0, 384)
-        finish(u3, 384, CH)
+        add_turned(s1, kept[u1], 0, CH, True)
+        add_turned(s1, mixed[u1], 0, CH, False)
+        empty(u1, 0, CH, s1)
+        pick_res(u2, 0, H)
+        pick_res(u2, H, CH)
+        diff(u3, 0, H, "d110")
+        t2 = new_bank("turn0")
+        turn_res(u2, 0, H, t2, 0)
+        t3 = new_bank("bank101")
+        turn_res(u2, H, CH, t3, 0)
+        keep_res(u2, 0, H, t2)
+        keep_res(u2, H, CH, t3)
+        diff(u3, H, CH, f"picked10{H}")
+        s2 = new_bank("bank010")
+        add_turned(s2, mixed[u2], 0, CH, True)
+        add_turned(s2, kept[u2], 0, CH, False)
+        empty(u2, 0, CH, s2)
+        gate(u3, 0, H, "th10")
+        gate(u3, H, CH, "e11")
+        finish(u3, 0, H)
+        finish(u3, H, CH)

@@ -181,11 +181,11 @@ def tile_picked_highway_gelu_p_kernel(tc, x_words, x_scales, res, w1, w2, offs, 
             m, c = u
             queue.dma_start(out=out[block(m), c * CH + a : c * CH + b], in_=piece[:])
 
-        def empty(u, a, b, bank):
+        def empty(u, a, b, bank, queue):
             m, c = u
             piece = keep.tile([P, b - a], F32, name=f"o{m}{c}{a}")
             nc.scalar.activation(piece[:], bank[:, 0 : b - a], ACT.Copy, scale=0.5)
-            store(u, a, b, piece, nc.scalar)
+            store(u, a, b, piece, queue)
 
         def diff(u, a, b, tag):
             m, c = u
@@ -198,10 +198,10 @@ def tile_picked_highway_gelu_p_kernel(tc, x_words, x_scales, res, w1, w2, offs, 
             e[u, a] = keep.tile([P, b - a], F32, name=f"e{m}{c}{a}", tag=tag)
             nc.vector.scalar_tensor_tensor(e[u, a][:], th[u][:, a:b], 1.0, d[u, a][:], ALU.add, ALU.mult)
 
-        def finish(u, a, b):
+        def finish(u, a, b, at):
             m, c = u
             piece = keep.tile([P, b - a], F32, name=f"o{m}{c}{a}")
-            nc.vector.scalar_tensor_tensor(piece[:], e[u, a][:], 0.5, y[u][:, a:b], ALU.mult, ALU.add)
+            nc.vector.scalar_tensor_tensor(piece[:], e[u, at][:, a - at : b - at], 0.5, y[u][:, a:b], ALU.mult, ALU.add)
             store(u, a, b, piece, nc.sync)
 
         u0, u1, u2, u3 = (0, 0), (0, 1), (1, 0), (1, 1)
@@ -212,47 +212,44 @@ def tile_picked_highway_gelu_p_kernel(tc, x_words, x_scales, res, w1, w2, offs, 
             z[i, u3] = product(i, u3)
         for u in (u0, u2, u1):
             gate_tanh(u)
-            complement_scalar(u)
+            (complement if u == u0 else complement_scalar)(u)
             layer(u)
             mix(u, f"mixed{u[0]}{u[1]}")
         layer(u3)
         H = CH // 2
-        for u in (u0, u1, u2):
-            kept[u] = sbuf("kept", u)
         pick_res(u0, 0, CH)
-        pick_res(u1, 0, H)
-        pick_res(u1, H, CH)
+        pick_res(u1, 0, CH)
         t0 = new_bank("turn0")
         turn_res(u0, 0, CH, t0, 0)
+        kept[u0] = sbuf("kept", u0)
         keep_res(u0, 0, CH, t0)
         t1 = new_bank("turn1")
-        turn_res(u1, 0, H, t1, 0)
-        turn_res(u1, H, CH, t1, H)
-        keep_res(u1, 0, CH, t1)
+        turn_res(u1, 0, CH, t1, 0)
         s0 = new_bank("bank110")
         add_turned(s0, mixed[u0], 0, CH, True)
         add_turned(s0, kept[u0], 0, CH, False)
-        empty(u0, 0, CH, s0)
-        s1 = new_bank("bank001")
-        gate_tanh(u3)
-        add_turned(s1, kept[u1], 0, CH, True)
-        add_turned(s1, mixed[u1], 0, CH, False)
-        empty(u1, 0, CH, s1)
+        empty(u0, 0, CH, s0, nc.sync)
         pick_res(u2, 0, H)
         pick_res(u2, H, CH)
-        diff(u3, 0, H, "d110")
         t2 = new_bank("turn0")
         turn_res(u2, 0, H, t2, 0)
         t3 = new_bank("bank101")
         turn_res(u2, H, CH, t3, 0)
+        kept[u1] = keep.tile([P, CH], F32, name="kept01", tag="picked100")
+        keep_res(u1, 0, CH, t1)
+        kept[u2] = sbuf("kept", u2)
         keep_res(u2, 0, H, t2)
         keep_res(u2, H, CH, t3)
-        diff(u3, H, CH, f"picked10{H}")
-        s2 = new_bank("bank010")
-        add_turned(s2, mixed[u2], 0, CH, True)
-        add_turned(s2, kept[u2], 0, CH, False)
-        empty(u2, 0, CH, s2)
-        gate(u3, 0, H, "th10")
+        gate_tanh(u3)
+        for u, tag, queue in ((u1, "bank001", nc.sync), (u2, "bank010", nc.scalar)):
+            s = new_bank(tag)
+            add_turned(s, mixed[u], 0, CH, True)
+            add_turned(s, kept[u], 0, CH, False)
+            empty(u, 0, CH, s, queue)
+        diff(u3, 0, H, f"picked10{H}")
+        diff(u3, H, CH, "th10")
+        gate(u3, 0, H, "e10")
         gate(u3, H, CH, "e11")
-        finish(u3, 0, H)
-        finish(u3, H, CH)
+        finish(u3, 0, H, 0)
+        finish(u3, H, 384, H)
+        finish(u3, 384, CH, H)

@@ -99,7 +99,7 @@ def tile_picked_highway_gelu_p_kernel(tc, x_words, x_scales, res, w1, w2, offs, 
 
         def product(i, u):
             m, c = u
-            acc = products.tile([P, CH], F32, name="acc", tag=f"bank{i}00")
+            acc = products.tile([P, CH], F32, name="acc", tag=f"turn{i}")
             nc.tensor.matmul_mx(
                 out=acc[:],
                 lhsT=codes[i][:, block(m)].bitcast(FP8X4),
@@ -138,7 +138,7 @@ def tile_picked_highway_gelu_p_kernel(tc, x_words, x_scales, res, w1, w2, offs, 
             nc.scalar.activation(th[u][:], z[1, u][:], ACT.Tanh, scale=-0.5)
 
         def complement(u):
-            rest[u] = sbuf("rest", u)
+            rest[u] = keep.tile([P, CH], F32, name="rest00", tag="grouped0", align_bytes=64)
             nc.gpsimd.tensor_scalar(rest[u][:], th[u][:], -1.0, 1.0, ALU.mult, ALU.add)
 
         def complement_scalar(u):
@@ -219,19 +219,19 @@ def tile_picked_highway_gelu_p_kernel(tc, x_words, x_scales, res, w1, w2, offs, 
         H = CH // 2
         pick_res(u0, 0, CH)
         pick_res(u1, 0, CH)
-        t0 = new_bank("turn0")
+        t0 = new_bank("bank100")
         turn_res(u0, 0, CH, t0, 0)
         kept[u0] = sbuf("kept", u0)
         keep_res(u0, 0, CH, t0)
-        t1 = new_bank("turn1")
+        t1 = new_bank("bank110")
         turn_res(u1, 0, CH, t1, 0)
-        s0 = new_bank("bank110")
+        s0 = new_bank("bank000")
         add_turned(s0, mixed[u0], 0, CH, True)
         add_turned(s0, kept[u0], 0, CH, False)
         empty(u0, 0, CH, s0, nc.sync)
         pick_res(u2, 0, H)
         pick_res(u2, H, CH)
-        t2 = new_bank("turn0")
+        t2 = new_bank("bank100")
         turn_res(u2, 0, H, t2, 0)
         t3 = new_bank("bank101")
         turn_res(u2, H, CH, t3, 0)
@@ -241,7 +241,7 @@ def tile_picked_highway_gelu_p_kernel(tc, x_words, x_scales, res, w1, w2, offs, 
         keep_res(u2, 0, H, t2)
         keep_res(u2, H, CH, t3)
         gate_tanh(u3)
-        for u, tag, queue in ((u1, "bank001", nc.sync), (u2, "bank010", nc.scalar)):
+        for u, tag, queue in ((u1, "bank001", nc.sync), (u2, "bank110", nc.scalar)):
             s = new_bank(tag)
             add_turned(s, mixed[u], 0, CH, True)
             add_turned(s, kept[u], 0, CH, False)

@@ -99,7 +99,7 @@ def tile_picked_highway_gelu_p_kernel(tc, x_words, x_scales, res, w1, w2, offs, 
 
         def product(i, u):
             m, c = u
-            acc = products.tile([P, CH], F32, name="acc", tag=f"turn{i}")
+            acc = products.tile([P, CH], F32, name="acc", tag=f"bank{i}{m}{c}")
             nc.tensor.matmul_mx(
                 out=acc[:],
                 lhsT=codes[i][:, block(m)].bitcast(FP8X4),
@@ -206,50 +206,50 @@ def tile_picked_highway_gelu_p_kernel(tc, x_words, x_scales, res, w1, w2, offs, 
 
         u0, u1, u2, u3 = (0, 0), (0, 1), (1, 0), (1, 1)
         z = {}
-        for i, u in ((1, u0), (1, u2), (0, u0), (0, u2), (1, u1), (0, u1)):
-            z[i, u] = product_turned(i, u)
+        z[1, u0] = product_turned(1, u0)
+        z[1, u2] = product(1, u2)
+        z[0, u0] = product_turned(0, u0)
+        z[0, u2] = product(0, u2)
+        for i in (1, 0):
+            z[i, u1] = product_turned(i, u1)
         for i in (0, 1):
             z[i, u3] = product(i, u3)
-        for u in (u0, u2, u1):
-            gate_tanh(u)
-            (complement if u == u0 else complement_scalar)(u)
-            layer(u)
-            mix(u, f"mixed{u[0]}{u[1]}")
+        gate_tanh(u0)
+        complement(u0)
+        gate_tanh(u2)
+        layer(u0)
+        mix(u0, "mixed00")
+        gate_tanh(u1)
+        complement_scalar(u1)
+        layer(u1)
+        mix(u1, "mixed01")
+        layer(u2)
         layer(u3)
         H = CH // 2
         pick_res(u0, 0, CH)
-        pick_res(u1, 0, CH)
+        pick_res(u1, 0, H)
+        pick_res(u1, H, CH)
         t0 = new_bank("bank100")
         turn_res(u0, 0, CH, t0, 0)
-        kept[u0] = sbuf("kept", u0)
-        keep_res(u0, 0, CH, t0)
         t1 = new_bank("bank110")
-        turn_res(u1, 0, CH, t1, 0)
-        s0 = new_bank("bank000")
-        add_turned(s0, mixed[u0], 0, CH, True)
-        add_turned(s0, kept[u0], 0, CH, False)
-        empty(u0, 0, CH, s0, nc.sync)
-        pick_res(u2, 0, H)
-        pick_res(u2, H, CH)
-        t2 = new_bank("bank100")
-        turn_res(u2, 0, H, t2, 0)
-        t3 = new_bank("bank101")
-        turn_res(u2, H, CH, t3, 0)
-        kept[u1] = keep.tile([P, CH], F32, name="kept01", tag="picked100")
-        keep_res(u1, 0, CH, t1)
-        kept[u2] = sbuf("kept", u2)
-        keep_res(u2, 0, H, t2)
-        keep_res(u2, H, CH, t3)
-        gate_tanh(u3)
-        for u, tag, queue in ((u1, "bank001", nc.sync), (u2, "bank110", nc.scalar)):
+        turn_res(u1, 0, H, t1, 0)
+        turn_res(u1, H, CH, t1, H)
+        for u, bank in ((u0, t0), (u1, t1)):
+            kept[u] = sbuf("kept", u)
+            keep_res(u, 0, CH, bank)
+        for u, tag in ((u0, "bank000"), (u1, "bank001")):
             s = new_bank(tag)
             add_turned(s, mixed[u], 0, CH, True)
             add_turned(s, kept[u], 0, CH, False)
-            empty(u, 0, CH, s, queue)
-        diff(u3, 0, H, f"picked10{H}")
-        diff(u3, H, CH, "th10")
-        gate(u3, 0, H, "e10")
-        gate(u3, H, CH, "e11")
+            empty(u, 0, CH, s, nc.scalar)
+        gate_tanh(u3)
+        diff(u2, 0, CH, "rest01")
+        diff(u3, 0, H, "th01")
+        gate(u2, 0, CH, "e10")
+        diff(u3, H, CH, "d11")
+        finish(u2, 0, CH, 0)
+        gate(u3, 0, H, "e110")
+        gate(u3, H, CH, "e111")
         finish(u3, 0, H, 0)
         finish(u3, H, 384, H)
         finish(u3, 384, CH, H)

@@ -129,9 +129,10 @@ def tile_picked_highway_gelu_p_kernel(tc, x_words, x_scales, res, w1, w2, offs, 
         def sbuf(kind, u):
             return keep.tile([P, CH], F32, name=f"{kind}{u[0]}{u[1]}")
 
-        def layer(u):
-            y[u] = sbuf("y", u)
-            nc.scalar.activation(y[u][:], z[0, u][:], ACT.Gelu_apprx_tanh)
+        def layer(u, a=0, b=CH):
+            if u not in y:
+                y[u] = sbuf("y", u)
+            nc.scalar.activation(y[u][:, a:b], z[0, u][:, a:b], ACT.Gelu_apprx_tanh)
 
         def gate_tanh(u):
             th[u] = sbuf("th", u)
@@ -141,13 +142,15 @@ def tile_picked_highway_gelu_p_kernel(tc, x_words, x_scales, res, w1, w2, offs, 
             rest[u] = keep.tile([P, CH], F32, name="rest00", tag="grouped0", align_bytes=64)
             nc.gpsimd.tensor_scalar(rest[u][:], th[u][:], -1.0, 1.0, ALU.mult, ALU.add)
 
-        def complement_scalar(u):
-            rest[u] = sbuf("rest", u)
-            nc.scalar.activation(rest[u][:], th[u][:], ACT.Identity, bias=1.0, scale=-1.0)
+        def complement_scalar(u, a, b):
+            if u not in rest:
+                rest[u] = sbuf("rest", u)
+            nc.scalar.activation(rest[u][:, a:b], th[u][:, a:b], ACT.Identity, bias=1.0, scale=-1.0)
 
-        def mix(u, tag):
-            mixed[u] = keep.tile([P, CH], F32, name=f"mixed{u[0]}{u[1]}", tag=tag)
-            nc.gpsimd.tensor_tensor(mixed[u][:], rest[u][:], y[u][:], ALU.mult)
+        def mix(u, a, b):
+            if u not in mixed:
+                mixed[u] = sbuf("mixed", u)
+            nc.gpsimd.tensor_tensor(mixed[u][:, a:b], rest[u][:, a:b], y[u][:, a:b], ALU.mult)
 
         def pick_res(u, a, b, tag=None):
             m, c = u
@@ -187,16 +190,15 @@ def tile_picked_highway_gelu_p_kernel(tc, x_words, x_scales, res, w1, w2, offs, 
             nc.scalar.activation(piece[:], bank[:, 0 : b - a], ACT.Copy, scale=0.5)
             store(u, a, b, piece, queue)
 
-        def diff(u, a, b, tag):
+        def diff(u, a, b, into):
             m, c = u
-            d[u, a] = keep.tile([P, b - a], F32, name=f"d{m}{c}{a}", tag=tag)
+            d[u, a] = into
             part = offsets[:, (c * CH + a) // PER_COL : (c * CH + b) // PER_COL]
-            nc.vector.tensor_tensor(d[u, a][:], res_rows[m][:].indirect(part), y[u][:, a:b], ALU.subtract)
+            nc.vector.tensor_tensor(into, res_rows[m][:].indirect(part), y[u][:, a:b], ALU.subtract)
 
-        def gate(u, a, b, tag):
-            m, c = u
-            e[u, a] = keep.tile([P, b - a], F32, name=f"e{m}{c}{a}", tag=tag)
-            nc.vector.scalar_tensor_tensor(e[u, a][:], th[u][:, a:b], 1.0, d[u, a][:], ALU.add, ALU.mult)
+        def gate(u, a, b, into):
+            e[u, a] = into
+            nc.vector.scalar_tensor_tensor(into, th[u][:, a:b], 1.0, d[u, a], ALU.add, ALU.mult)
 
         def finish(u, a, b, at):
             m, c = u
@@ -218,14 +220,16 @@ def tile_picked_highway_gelu_p_kernel(tc, x_words, x_scales, res, w1, w2, offs, 
         complement(u0)
         gate_tanh(u2)
         layer(u0)
-        mix(u0, "mixed00")
-        gate_tanh(u1)
-        complement_scalar(u1)
-        layer(u1)
-        mix(u1, "mixed01")
+        mix(u0, 0, CH)
         layer(u2)
-        layer(u3)
+        gate_tanh(u1)
         H = CH // 2
+        for a in (0, H):
+            complement_scalar(u1, a, a + H)
+            layer(u1, a, a + H)
+            mix(u1, a, a + H)
+        layer(u3)
+        gate_tanh(u3)
         pick_res(u0, 0, CH)
         pick_res(u1, 0, H)
         pick_res(u1, H, CH)
@@ -233,23 +237,32 @@ def tile_picked_highway_gelu_p_kernel(tc, x_words, x_scales, res, w1, w2, offs, 
         turn_res(u0, 0, CH, t0, 0)
         t1 = new_bank("bank110")
         turn_res(u1, 0, H, t1, 0)
-        turn_res(u1, H, CH, t1, H)
-        for u, bank in ((u0, t0), (u1, t1)):
+        t2 = new_bank("bank010")
+        turn_res(u1, H, CH, t2, 0)
+        for u in (u0, u1):
             kept[u] = sbuf("kept", u)
-            keep_res(u, 0, CH, bank)
+        keep_res(u0, 0, CH, t0)
+        keep_res(u1, 0, H, t1)
+        keep_res(u1, H, CH, t2)
         for u, tag in ((u0, "bank000"), (u1, "bank001")):
             s = new_bank(tag)
             add_turned(s, mixed[u], 0, CH, True)
             add_turned(s, kept[u], 0, CH, False)
             empty(u, 0, CH, s, nc.scalar)
-        gate_tanh(u3)
-        diff(u2, 0, CH, "rest01")
-        diff(u3, 0, H, "th01")
-        gate(u2, 0, CH, "e10")
-        diff(u3, H, CH, "d11")
+        first = keep.tile([P, H], F32, name="first", tag="picked01256")
+        held = keep.tile([P, CH + H], F32, name="held", tag="rest01")
+        gated = keep.tile([P, 2 * CH], F32, name="gated")
+        diff(u2, 0, H, first[:])
+        diff(u2, H, CH, held[:, 0:H])
+        diff(u3, 0, CH, held[:, H : H + CH])
+        gate(u2, 0, H, gated[:, 0:H])
+        gate(u2, H, CH, gated[:, H:CH])
+        e[u2, 0] = gated[:, 0:CH]
+        d[u3, H] = held[:, CH : CH + H]
+        d[u3, 0] = held[:, H:CH]
+        gate(u3, 0, H, gated[:, CH : CH + H])
         finish(u2, 0, CH, 0)
-        gate(u3, 0, H, "e110")
-        gate(u3, H, CH, "e111")
+        gate(u3, H, CH, gated[:, CH + H : 2 * CH])
         finish(u3, 0, H, 0)
         finish(u3, H, 384, H)
         finish(u3, 384, CH, H)

@@ -59,9 +59,6 @@ def tile_picked_highway_gelu_p_kernel(tc, x_words, x_scales, res, w1, w2, offs, 
             nc.sync.dma_start(out=r[:], in_=res[m * P : (m + 1) * P, :])
             res_rows.append(r)
 
-        def entries(c):
-            return offsets[:, c * CH // PER_COL : (c + 1) * CH // PER_COL]
-
         grouped, codes, scales = {}, {}, {}
         for i in (1, 0):
             grouped[i] = keep.tile([P, N * PACK], BF16, name=f"grouped{i}", align_bytes=64)
@@ -75,68 +72,76 @@ def tile_picked_highway_gelu_p_kernel(tc, x_words, x_scales, res, w1, w2, offs, 
         def quantize(i):
             nc.vector.quantize_mx(out=codes[i][:].bitcast(FP8X4), scales=scales[i][:], in_=grouped[i][:])
 
-        picked_words, picked_scales = {}, {}
+        H = CH // 2
 
-        def pick_words(c, tag):
-            picked_words[c] = keep.tile([P, CH], U16, name=f"picked_words{c}", tag=tag, align_bytes=64)
-            nc.vector.tensor_copy(picked_words[c][:], word_table[:].indirect(entries(c)))
+        def span(a, b):
+            return offsets[:, a // PER_COL : b // PER_COL]
 
-        def pick_scales(c, tag):
-            picked_scales[c] = keep.tile([P, CH], U8, name=f"picked_scales{c}", tag=tag, align_bytes=64)
-            nc.vector.tensor_copy(picked_scales[c][:], scale_table[:].indirect(entries(c)))
+        def pick_words(a, b, tag):
+            t = keep.tile([P, b - a], U16, name=f"picked_words{a}", tag=tag, align_bytes=64)
+            nc.vector.tensor_copy(t[:], word_table[:].indirect(span(a, b)))
+            return t
 
-        pick_words(0, "picked_words0")
-        pick_scales(0, "picked_scales0")
+        words0 = pick_words(0, CH, "picked_words0")
+        bytes0 = keep.tile([P, CH], U8, name="bytes0", align_bytes=64)
+        nc.vector.tensor_copy(bytes0[:], scale_table[:].indirect(span(0, CH)))
+        words1 = [pick_words(CH, CH + H, "picked_words1")]
         quantize(1)
-        pick_words(1, "raw1")
+        words1.append(pick_words(CH + H, S, "raw1"))
         quantize(0)
-        pick_scales(1, "raw0")
+        bytes1 = keep.tile([P, CH], U8, name="bytes1", tag="raw0", align_bytes=64)
+        for a in (0, H):
+            nc.vector.tensor_copy(bytes1[:, a : a + H], scale_table[:].indirect(span(CH + a, CH + a + H)))
+
+        def tokens(c, a, b):
+            if c == 0:
+                return words0[:, a:b].bitcast(FP4X4), bytes0[:, a:b]
+            return words1[a // H][:, a % H : a % H + b - a].bitcast(FP4X4), bytes1[:, a:b]
 
         y, th, rest, mixed, picked, kept, total, d, e = {}, {}, {}, {}, {}, {}, {}, {}, {}
 
         def block(b):
             return slice(b * P, (b + 1) * P)
 
-        def product(i, u):
+        def product(i, u, acc, a, b):
             m, c = u
-            acc = products.tile([P, CH], F32, name="acc", tag=f"bank{i}{m}{c}")
+            words, scale = tokens(c, a, b)
             nc.tensor.matmul_mx(
-                out=acc[:],
+                out=acc,
                 lhsT=codes[i][:, block(m)].bitcast(FP8X4),
                 lhsT_scale=scales[i][:, block(m)],
-                rhs=picked_words[c][:].bitcast(FP4X4),
-                rhs_scale=picked_scales[c][:],
+                rhs=words,
+                rhs_scale=scale,
                 start=True,
                 stop=True,
             )
-            return acc
 
-        def product_turned(i, u):
+        def product_turned(i, u, acc, a, b):
             m, c = u
-            acc = products.tile([P, CH], F32, name="acc", tag=f"bank{i}{m}{c}")
-            for b in range(BLOCKS):
+            for k in range((b - a) // P):
+                words, scale = tokens(c, a + k * P, a + (k + 1) * P)
                 nc.tensor.matmul_mx(
-                    out=acc[:, block(b)],
-                    lhsT=picked_words[c][:, block(b)].bitcast(FP4X4),
-                    lhsT_scale=picked_scales[c][:, block(b)],
+                    out=acc[:, block(k)],
+                    lhsT=words,
+                    lhsT_scale=scale,
                     rhs=codes[i][:, block(m)].bitcast(FP8X4),
                     rhs_scale=scales[i][:, block(m)],
                     start=True,
                     stop=True,
                 )
-            return acc
 
         def sbuf(kind, u):
             return keep.tile([P, CH], F32, name=f"{kind}{u[0]}{u[1]}")
 
-        def layer(u, a=0, b=CH):
+        def layer(u, src, a=0, b=CH):
             if u not in y:
                 y[u] = sbuf("y", u)
-            nc.scalar.activation(y[u][:, a:b], z[0, u][:, a:b], ACT.Gelu_apprx_tanh)
+            nc.scalar.activation(y[u][:, a:b], src, ACT.Gelu_apprx_tanh)
 
-        def gate_tanh(u):
-            th[u] = sbuf("th", u)
-            nc.scalar.activation(th[u][:], z[1, u][:], ACT.Tanh, scale=-0.5)
+        def gate_tanh(u, src, a=0, b=CH):
+            if u not in th:
+                th[u] = sbuf("th", u)
+            nc.scalar.activation(th[u][:, a:b], src, ACT.Tanh, scale=-0.5)
 
         def complement(u):
             rest[u] = keep.tile([P, CH], F32, name="rest00", tag="grouped0", align_bytes=64)
@@ -207,44 +212,49 @@ def tile_picked_highway_gelu_p_kernel(tc, x_words, x_scales, res, w1, w2, offs, 
             store(u, a, b, piece, nc.sync)
 
         u0, u1, u2, u3 = (0, 0), (0, 1), (1, 0), (1, 1)
-        z = {}
-        z[1, u0] = product_turned(1, u0)
-        z[1, u2] = product(1, u2)
-        z[0, u0] = product_turned(0, u0)
-        z[0, u2] = product(0, u2)
-        for i in (1, 0):
-            z[i, u1] = product_turned(i, u1)
-        for i in (0, 1):
-            z[i, u3] = product(i, u3)
-        gate_tanh(u0)
+        g0, g2, l0 = new_bank("A"), new_bank("B"), new_bank("C")
+        product_turned(1, u0, g0[:], 0, CH)
+        product(1, u2, g2[:], 0, CH)
+        product_turned(0, u0, l0[:], 0, CH)
+        halves = [new_bank("D"), new_bank("E")]
+        for a, bank in zip((0, H), halves):
+            product_turned(1, u1, bank[:, 0:H], a, a + H)
+            product_turned(0, u1, bank[:, H:CH], a, a + H)
+        l2 = new_bank("F")
+        product(0, u2, l2[:], 0, CH)
+        gate_tanh(u0, g0[:])
         complement(u0)
-        gate_tanh(u2)
-        layer(u0)
+        gate_tanh(u2, g2[:])
+        layer(u0, l0[:])
         mix(u0, 0, CH)
-        layer(u2)
-        gate_tanh(u1)
-        H = CH // 2
-        for a in (0, H):
+        for a, bank in zip((0, H), halves):
+            gate_tanh(u1, bank[:, 0:H], a, a + H)
             complement_scalar(u1, a, a + H)
-            layer(u1, a, a + H)
+            layer(u1, bank[:, H:CH], a, a + H)
             mix(u1, a, a + H)
-        layer(u3)
-        gate_tanh(u3)
+        layer(u2, l2[:])
         pick_res(u0, 0, CH)
         pick_res(u1, 0, H)
         pick_res(u1, H, CH)
-        t0 = new_bank("bank100")
+        t0 = new_bank("A")
         turn_res(u0, 0, CH, t0, 0)
-        t1 = new_bank("bank110")
+        l3, g3 = new_bank("G"), new_bank("H")
+        for a in (0, H):
+            product(0, u3, l3[:, a : a + H], a, a + H)
+        layer(u3, l3[:])
+        t1 = new_bank("B")
         turn_res(u1, 0, H, t1, 0)
-        t2 = new_bank("bank010")
+        t2 = new_bank("D")
         turn_res(u1, H, CH, t2, 0)
+        for a in (0, H):
+            product(1, u3, g3[:, a : a + H], a, a + H)
+        gate_tanh(u3, g3[:])
         for u in (u0, u1):
             kept[u] = sbuf("kept", u)
         keep_res(u0, 0, CH, t0)
         keep_res(u1, 0, H, t1)
         keep_res(u1, H, CH, t2)
-        for u, tag in ((u0, "bank000"), (u1, "bank001")):
+        for u, tag in ((u0, "C"), (u1, "E")):
             s = new_bank(tag)
             add_turned(s, mixed[u], 0, CH, True)
             add_turned(s, kept[u], 0, CH, False)

@@ -61,16 +61,19 @@ def tile_picked_highway_gelu_p_kernel(tc, x_words, x_scales, res, w1, w2, offs, 
 
         grouped, codes, scales = {}, {}, {}
         for i in (1, 0):
-            grouped[i] = keep.tile([P, N * PACK], BF16, name=f"grouped{i}", align_bytes=64)
             codes[i] = keep.tile([P, N], U32, name=f"codes{i}", align_bytes=64)
             scales[i] = keep.tile([P, N], U8, name=f"scales{i}", align_bytes=64)
-            nc.scalar.copy(
-                out=grouped[i][:].rearrange("p (c i t) -> p c t i", i=4, t=PACK),
-                in_=raw[i][:].rearrange("p t (c i) -> p c t i", i=4),
-            )
+            for m in range(N // P):
+                grouped[i, m] = keep.tile([P, P * PACK], BF16, name=f"grouped{i}{m}", align_bytes=64)
+                nc.scalar.copy(
+                    out=grouped[i, m][:].rearrange("p (c i t) -> p c t i", i=4, t=PACK),
+                    in_=raw[i][:, :, m * P : (m + 1) * P].rearrange("p t (c i) -> p c t i", i=4),
+                )
 
         def quantize(i):
-            nc.vector.quantize_mx(out=codes[i][:].bitcast(FP8X4), scales=scales[i][:], in_=grouped[i][:])
+            for m in range(N // P):
+                cols = slice(m * P, (m + 1) * P)
+                nc.vector.quantize_mx(out=codes[i][:, cols].bitcast(FP8X4), scales=scales[i][:, cols], in_=grouped[i, m][:])
 
         H = CH // 2
 
@@ -144,7 +147,7 @@ def tile_picked_highway_gelu_p_kernel(tc, x_words, x_scales, res, w1, w2, offs, 
             nc.scalar.activation(th[u][:, a:b], src, ACT.Tanh, scale=-0.5)
 
         def complement(u):
-            rest[u] = keep.tile([P, CH], F32, name="rest00", tag="grouped0", align_bytes=64)
+            rest[u] = keep.tile([P, CH], F32, name="rest00", tag="grouped01", align_bytes=64)
             nc.gpsimd.tensor_scalar(rest[u][:], th[u][:], -1.0, 1.0, ALU.mult, ALU.add)
 
         def complement_scalar(u, a, b):
@@ -259,17 +262,13 @@ def tile_picked_highway_gelu_p_kernel(tc, x_words, x_scales, res, w1, w2, offs, 
             add_turned(s, mixed[u], 0, CH, True)
             add_turned(s, kept[u], 0, CH, False)
             empty(u, 0, CH, s, nc.scalar)
-        first = keep.tile([P, H], F32, name="first", tag="picked01256")
-        held = keep.tile([P, CH + H], F32, name="held", tag="rest01")
+        held = keep.tile([P, 2 * CH], F32, name="held", tag="picked01256")
         gated = keep.tile([P, 2 * CH], F32, name="gated")
-        diff(u2, 0, H, first[:])
-        diff(u2, H, CH, held[:, 0:H])
-        diff(u3, 0, CH, held[:, H : H + CH])
-        gate(u2, 0, H, gated[:, 0:H])
-        gate(u2, H, CH, gated[:, H:CH])
-        e[u2, 0] = gated[:, 0:CH]
-        d[u3, H] = held[:, CH : CH + H]
-        d[u3, 0] = held[:, H:CH]
+        diff(u2, 0, CH, held[:, 0:CH])
+        diff(u3, 0, CH, held[:, CH : 2 * CH])
+        gate(u2, 0, CH, gated[:, 0:CH])
+        d[u3, H] = held[:, CH + H : 2 * CH]
+        d[u3, 0] = held[:, CH : CH + H]
         gate(u3, 0, H, gated[:, CH : CH + H])
         finish(u2, 0, CH, 0)
         gate(u3, H, CH, gated[:, CH + H : 2 * CH])

@@ -19,16 +19,24 @@ ALU = mybir.AluOpType
 
 P = 128
 PACK = 4
-CH = 512
+RUN = 4
+QUADRANT = 32
+SCALE_ROWS = 4
 PER_COL = 16
+CH = 512
+H = CH // 2
 BLOCKS = CH // P
+LAYER, GATE = 0, 1
 
 
 def tile_picked_highway_gelu_p_kernel(tc, x_words, x_scales, res, w1, w2, offs, out):
     nc = tc.nc
     with ExitStack() as ctx:
         keep = ctx.enter_context(tc.tile_pool(name="keep", bufs=1))
-        products = ctx.enter_context(tc.psum_pool(name="products", bufs=1))
+        psum = ctx.enter_context(tc.psum_pool(name="psum", bufs=1))
+
+        def block(b):
+            return slice(b * P, (b + 1) * P)
 
         word_table = keep.tile([P, T], U16, name="word_table", align_bytes=64)
         nc.sync.dma_start(out=word_table[:].bitcast(I32), in_=x_words[0].bitcast(I32))
@@ -41,150 +49,135 @@ def tile_picked_highway_gelu_p_kernel(tc, x_words, x_scales, res, w1, w2, offs, 
         warm_out = keep.tile([P, 1], F32, name="warm_out")
         nc.gpsimd.memset(warm_in[:], 0.0)
         nc.scalar.activation(warm_out[:], warm_in[:], ACT.Gelu_apprx_tanh)
-        for q in range(4):
+        for q in range(P // QUADRANT):
             nc.sync.dma_start(
-                out=scale_table[32 * q : 32 * q + 4, :].bitcast(I32),
-                in_=x_scales[0, 4 * q : 4 * q + 4, :].bitcast(I32),
+                out=scale_table[QUADRANT * q : QUADRANT * q + SCALE_ROWS, :].bitcast(I32),
+                in_=x_scales[0, SCALE_ROWS * q : SCALE_ROWS * (q + 1), :].bitcast(I32),
             )
         identity = keep.tile([P, P], F32, name="identity")
         make_identity(nc, identity[:])
 
         raw = {}
-        for i, w in ((1, w2), (0, w1)):
+        for i, w in ((GATE, w2), (LAYER, w1)):
             raw[i] = keep.tile([P, PACK, N], F32, name=f"raw{i}", align_bytes=64)
-            nc.sync.dma_start(out=raw[i][:], in_=w.rearrange("(p j) c -> p j c", j=PACK))
+            nc.sync.dma_start(out=raw[i][:], in_=w.rearrange("(p t) c -> p t c", t=PACK))
         res_rows = []
         for m in range(N // P):
-            r = keep.tile([P, T], F32, name=f"res_rows{m}")
-            nc.sync.dma_start(out=r[:], in_=res[m * P : (m + 1) * P, :])
-            res_rows.append(r)
+            rows = keep.tile([P, T], F32, name=f"res_rows{m}")
+            nc.sync.dma_start(out=rows[:], in_=res[block(m), :])
+            res_rows.append(rows)
 
         grouped, codes, scales = {}, {}, {}
-        for i in (1, 0):
+        for i in (GATE, LAYER):
             codes[i] = keep.tile([P, N], U32, name=f"codes{i}", align_bytes=64)
             scales[i] = keep.tile([P, N], U8, name=f"scales{i}", align_bytes=64)
             for m in range(N // P):
                 grouped[i, m] = keep.tile([P, P * PACK], BF16, name=f"grouped{i}{m}", align_bytes=64)
                 nc.scalar.copy(
-                    out=grouped[i, m][:].rearrange("p (c i t) -> p c t i", i=4, t=PACK),
-                    in_=raw[i][:, :, m * P : (m + 1) * P].rearrange("p t (c i) -> p c t i", i=4),
+                    out=grouped[i, m][:].rearrange("p (c r t) -> p c t r", r=RUN, t=PACK),
+                    in_=raw[i][:, :, block(m)].rearrange("p t (c r) -> p c t r", r=RUN),
                 )
 
         def quantize(i):
             for m in range(N // P):
-                cols = slice(m * P, (m + 1) * P)
-                nc.vector.quantize_mx(out=codes[i][:, cols].bitcast(FP8X4), scales=scales[i][:, cols], in_=grouped[i, m][:])
+                nc.vector.quantize_mx(
+                    out=codes[i][:, block(m)].bitcast(FP8X4), scales=scales[i][:, block(m)], in_=grouped[i, m][:]
+                )
 
-        H = CH // 2
-
-        def span(a, b):
+        def entries(a, b):
             return offsets[:, a // PER_COL : b // PER_COL]
 
         def pick_words(a, b, tag):
-            t = keep.tile([P, b - a], U16, name=f"picked_words{a}", tag=tag, align_bytes=64)
-            nc.vector.tensor_copy(t[:], word_table[:].indirect(span(a, b)))
-            return t
+            picked_words = keep.tile([P, b - a], U16, name=f"words{a}", tag=tag, align_bytes=64)
+            nc.vector.tensor_copy(picked_words[:], word_table[:].indirect(entries(a, b)))
+            return picked_words
 
-        words0 = pick_words(0, CH, "picked_words0")
+        words0 = pick_words(0, CH, "words_first")
         bytes0 = keep.tile([P, CH], U8, name="bytes0", align_bytes=64)
-        nc.vector.tensor_copy(bytes0[:], scale_table[:].indirect(span(0, CH)))
-        words1 = [pick_words(CH, CH + H, "picked_words1")]
-        quantize(1)
-        words1.append(pick_words(CH + H, S, "raw1"))
-        quantize(0)
-        bytes1 = keep.tile([P, CH], U8, name="bytes1", tag="raw0", align_bytes=64)
+        nc.vector.tensor_copy(bytes0[:], scale_table[:].indirect(entries(0, CH)))
+        words1 = [pick_words(CH, CH + H, "words_second")]
+        quantize(GATE)
+        words1.append(pick_words(CH + H, S, f"raw{GATE}"))
+        quantize(LAYER)
+        bytes1 = keep.tile([P, CH], U8, name="bytes1", tag=f"raw{LAYER}", align_bytes=64)
         for a in (0, H):
-            nc.vector.tensor_copy(bytes1[:, a : a + H], scale_table[:].indirect(span(CH + a, CH + a + H)))
+            nc.vector.tensor_copy(bytes1[:, a : a + H], scale_table[:].indirect(entries(CH + a, CH + a + H)))
 
         def tokens(c, a, b):
             if c == 0:
                 return words0[:, a:b].bitcast(FP4X4), bytes0[:, a:b]
             return words1[a // H][:, a % H : a % H + b - a].bitcast(FP4X4), bytes1[:, a:b]
 
-        y, th, rest, mixed, picked, kept, total, d, e = {}, {}, {}, {}, {}, {}, {}, {}, {}
+        y, th, rest, mixed, picked, kept = {}, {}, {}, {}, {}, {}
 
-        def block(b):
-            return slice(b * P, (b + 1) * P)
+        def bank(tag):
+            return psum.tile([P, CH], F32, name="bank", tag=tag)
+
+        def quarter_tile(kind, u):
+            return keep.tile([P, CH], F32, name=f"{kind}{u[0]}{u[1]}")
 
         def product(i, u, acc, a, b):
             m, c = u
-            words, scale = tokens(c, a, b)
+            words, scale_bytes = tokens(c, a, b)
             nc.tensor.matmul_mx(
                 out=acc,
                 lhsT=codes[i][:, block(m)].bitcast(FP8X4),
                 lhsT_scale=scales[i][:, block(m)],
                 rhs=words,
-                rhs_scale=scale,
+                rhs_scale=scale_bytes,
                 start=True,
                 stop=True,
             )
 
         def product_turned(i, u, acc, a, b):
             m, c = u
-            for k in range((b - a) // P):
-                words, scale = tokens(c, a + k * P, a + (k + 1) * P)
+            for n in range((b - a) // P):
+                words, scale_bytes = tokens(c, a + n * P, a + (n + 1) * P)
                 nc.tensor.matmul_mx(
-                    out=acc[:, block(k)],
+                    out=acc[:, block(n)],
                     lhsT=words,
-                    lhsT_scale=scale,
+                    lhsT_scale=scale_bytes,
                     rhs=codes[i][:, block(m)].bitcast(FP8X4),
                     rhs_scale=scales[i][:, block(m)],
                     start=True,
                     stop=True,
                 )
 
-        def sbuf(kind, u):
-            return keep.tile([P, CH], F32, name=f"{kind}{u[0]}{u[1]}")
-
-        def layer(u, src, a=0, b=CH):
+        def layer(u, src, a, b):
             if u not in y:
-                y[u] = sbuf("y", u)
+                y[u] = quarter_tile("y", u)
             nc.scalar.activation(y[u][:, a:b], src, ACT.Gelu_apprx_tanh)
 
-        def gate_tanh(u, src, a=0, b=CH):
+        def gate_tanh(u, src, a, b):
             if u not in th:
-                th[u] = sbuf("th", u)
+                th[u] = quarter_tile("th", u)
             nc.scalar.activation(th[u][:, a:b], src, ACT.Tanh, scale=-0.5)
-
-        def complement(u):
-            rest[u] = keep.tile([P, CH], F32, name="rest00", tag="grouped01", align_bytes=64)
-            nc.gpsimd.tensor_scalar(rest[u][:], th[u][:], -1.0, 1.0, ALU.mult, ALU.add)
-
-        def complement_scalar(u, a, b):
-            if u not in rest:
-                rest[u] = sbuf("rest", u)
-            nc.scalar.activation(rest[u][:, a:b], th[u][:, a:b], ACT.Identity, bias=1.0, scale=-1.0)
 
         def mix(u, a, b):
             if u not in mixed:
-                mixed[u] = sbuf("mixed", u)
+                mixed[u] = quarter_tile("mixed", u)
             nc.gpsimd.tensor_tensor(mixed[u][:, a:b], rest[u][:, a:b], y[u][:, a:b], ALU.mult)
 
-        def pick_res(u, a, b, tag=None):
+        def pick_res(u, a, b):
             m, c = u
-            picked[u, a] = keep.tile([P, b - a], F32, name=f"picked{m}{c}{a}", tag=tag or f"picked{m}{c}{a}")
-            part = offsets[:, (c * CH + a) // PER_COL : (c * CH + b) // PER_COL]
-            nc.vector.tensor_copy(picked[u, a][:], res_rows[m][:].indirect(part))
+            picked[u, a] = keep.tile([P, b - a], F32, name=f"picked{m}{c}{a}")
+            nc.vector.tensor_copy(picked[u, a][:], res_rows[m][:].indirect(entries(c * CH + a, c * CH + b)))
 
-        def turn_res(u, a, b, bank, at):
-            for k in range((b - a) // P):
-                nc.tensor.transpose(bank[:, at + k * P : at + (k + 1) * P], picked[u, a][:, block(k)], identity[:])
+        def turn_res(u, a, b, dst):
+            for n in range((b - a) // P):
+                nc.tensor.transpose(dst[:, block(n)], picked[u, a][:, block(n)], identity[:])
 
-        def new_bank(tag):
-            return products.tile([P, CH], F32, name="bank", tag=tag)
+        def keep_res(u, a, b, src):
+            nc.vector.scalar_tensor_tensor(kept[u][:, a:b], th[u][:, a:b], 1.0, src[:, 0 : b - a], ALU.add, ALU.mult)
 
-        def keep_res(u, a, b, bank):
-            nc.vector.scalar_tensor_tensor(kept[u][:, a:b], th[u][:, a:b], 1.0, bank[:, 0 : b - a], ALU.add, ALU.mult)
-
-        def add_turned(bank, src, a, b, first):
-            n = (b - a) // P
-            for k in range(n):
+        def add_turned(dst, src, blocks, opens, closes):
+            for n in blocks:
                 nc.tensor.matmul(
-                    bank[:, block(k)],
-                    src[:, a + k * P : a + (k + 1) * P],
+                    dst[:, block(n)],
+                    src[:, block(n)],
                     identity[:],
-                    start=(first and k == 0),
-                    stop=(not first and k == n - 1),
+                    start=(opens and n == blocks[0]),
+                    stop=(closes and n == blocks[-1]),
                     is_transpose=True,
                 )
 
@@ -192,86 +185,93 @@ def tile_picked_highway_gelu_p_kernel(tc, x_words, x_scales, res, w1, w2, offs, 
             m, c = u
             queue.dma_start(out=out[block(m), c * CH + a : c * CH + b], in_=piece[:])
 
-        def empty(u, a, b, bank, queue):
-            m, c = u
-            piece = keep.tile([P, b - a], F32, name=f"o{m}{c}{a}")
-            nc.scalar.activation(piece[:], bank[:, 0 : b - a], ACT.Copy, scale=0.5)
-            store(u, a, b, piece, queue)
+        def empty(u, src):
+            piece = quarter_tile("result", u)
+            nc.scalar.activation(piece[:], src[:], ACT.Copy, scale=0.5)
+            store(u, 0, CH, piece, nc.scalar)
 
-        def diff(u, a, b, into):
+        def difference(u, dst):
             m, c = u
-            d[u, a] = into
-            part = offsets[:, (c * CH + a) // PER_COL : (c * CH + b) // PER_COL]
-            nc.vector.tensor_tensor(into, res_rows[m][:].indirect(part), y[u][:, a:b], ALU.subtract)
+            nc.vector.tensor_tensor(dst, res_rows[m][:].indirect(entries(c * CH, (c + 1) * CH)), y[u][:], ALU.subtract)
 
-        def gate(u, a, b, into):
-            e[u, a] = into
-            nc.vector.scalar_tensor_tensor(into, th[u][:, a:b], 1.0, d[u, a], ALU.add, ALU.mult)
+        def gate(u, a, b, dst, src):
+            nc.vector.scalar_tensor_tensor(dst[:, a:b], th[u][:, a:b], 1.0, src[:, a:b], ALU.add, ALU.mult)
 
-        def finish(u, a, b, at):
-            m, c = u
-            piece = keep.tile([P, b - a], F32, name=f"o{m}{c}{a}")
-            nc.vector.scalar_tensor_tensor(piece[:], e[u, at][:, a - at : b - at], 0.5, y[u][:, a:b], ALU.mult, ALU.add)
+        def finish(u, a, b, src):
+            piece = keep.tile([P, b - a], F32, name=f"result{u[0]}{u[1]}{a}")
+            nc.vector.scalar_tensor_tensor(piece[:], src[:, a:b], 0.5, y[u][:, a:b], ALU.mult, ALU.add)
             store(u, a, b, piece, nc.sync)
 
-        u0, u1, u2, u3 = (0, 0), (0, 1), (1, 0), (1, 1)
-        g0, g2, l0 = new_bank("A"), new_bank("B"), new_bank("C")
-        product_turned(1, u0, g0[:], 0, CH)
-        product(1, u2, g2[:], 0, CH)
-        product_turned(0, u0, l0[:], 0, CH)
-        halves = [new_bank("D"), new_bank("E")]
-        for a, bank in zip((0, H), halves):
-            product_turned(1, u1, bank[:, 0:H], a, a + H)
-            product_turned(0, u1, bank[:, H:CH], a, a + H)
-        l2 = new_bank("F")
-        product(0, u2, l2[:], 0, CH)
-        gate_tanh(u0, g0[:])
-        complement(u0)
-        gate_tanh(u2, g2[:])
-        layer(u0, l0[:])
-        mix(u0, 0, CH)
-        for a, bank in zip((0, H), halves):
-            gate_tanh(u1, bank[:, 0:H], a, a + H)
-            complement_scalar(u1, a, a + H)
-            layer(u1, bank[:, H:CH], a, a + H)
-            mix(u1, a, a + H)
-        layer(u2, l2[:])
-        pick_res(u0, 0, CH)
-        pick_res(u1, 0, H)
-        pick_res(u1, H, CH)
-        t0 = new_bank("A")
-        turn_res(u0, 0, CH, t0, 0)
-        l3, g3 = new_bank("G"), new_bank("H")
+        turned0, turned1, plain0, plain1 = (0, 0), (0, 1), (1, 0), (1, 1)
+
+        gate_t0, gate_p0, layer_t0 = bank("A"), bank("B"), bank("C")
+        product_turned(GATE, turned0, gate_t0[:], 0, CH)
+        product(GATE, plain0, gate_p0[:], 0, CH)
+        product_turned(LAYER, turned0, layer_t0[:], 0, CH)
+        both_t1 = {0: bank("D"), H: bank("E")}
         for a in (0, H):
-            product(0, u3, l3[:, a : a + H], a, a + H)
-        layer(u3, l3[:])
-        t1 = new_bank("B")
-        turn_res(u1, 0, H, t1, 0)
-        t2 = new_bank("D")
-        turn_res(u1, H, CH, t2, 0)
+            product_turned(GATE, turned1, both_t1[a][:, 0:H], a, a + H)
+            product_turned(LAYER, turned1, both_t1[a][:, H:CH], a, a + H)
+        layer_p0 = bank("F")
+        product(LAYER, plain0, layer_p0[:], 0, CH)
+
+        gate_tanh(turned0, gate_t0[:], 0, CH)
+        rest[turned0] = keep.tile([P, CH], F32, name="rest00", tag=f"grouped{LAYER}1", align_bytes=64)
+        nc.gpsimd.tensor_scalar(rest[turned0][:], th[turned0][:], -1.0, 1.0, ALU.mult, ALU.add)
+        gate_tanh(plain0, gate_p0[:], 0, CH)
+        layer(turned0, layer_t0[:], 0, CH)
+        mix(turned0, 0, CH)
         for a in (0, H):
-            product(1, u3, g3[:, a : a + H], a, a + H)
-        gate_tanh(u3, g3[:])
-        for u in (u0, u1):
-            kept[u] = sbuf("kept", u)
-        keep_res(u0, 0, CH, t0)
-        keep_res(u1, 0, H, t1)
-        keep_res(u1, H, CH, t2)
-        for u, tag in ((u0, "C"), (u1, "E")):
-            s = new_bank(tag)
-            add_turned(s, mixed[u], 0, CH, True)
-            add_turned(s, kept[u], 0, CH, False)
-            empty(u, 0, CH, s, nc.scalar)
-        held = keep.tile([P, 2 * CH], F32, name="held", tag="picked01256")
+            gate_tanh(turned1, both_t1[a][:, 0:H], a, a + H)
+            if a == 0:
+                rest[turned1] = quarter_tile("rest", turned1)
+            nc.scalar.activation(
+                rest[turned1][:, a : a + H], th[turned1][:, a : a + H], ACT.Identity, bias=1.0, scale=-1.0
+            )
+            layer(turned1, both_t1[a][:, H:CH], a, a + H)
+            mix(turned1, a, a + H)
+        layer(plain0, layer_p0[:], 0, CH)
+
+        pick_res(turned0, 0, CH)
+        pick_res(turned1, 0, H)
+        pick_res(turned1, H, CH)
+        res_t0 = bank("A")
+        turn_res(turned0, 0, CH, res_t0)
+        layer_p1, gate_p1 = bank("G"), bank("H")
+        for a in (0, H):
+            product(LAYER, plain1, layer_p1[:, a : a + H], a, a + H)
+        layer(plain1, layer_p1[:], 0, CH)
+        res_t1 = {0: bank("B")}
+        turn_res(turned1, 0, H, res_t1[0])
+        sum_t0 = bank("C")
+        add_turned(sum_t0, mixed[turned0], range(BLOCKS), True, False)
+        res_t1[H] = bank("E")
+        turn_res(turned1, H, CH, res_t1[H])
+        sum_t1 = bank("D")
+        add_turned(sum_t1, mixed[turned1], range(BLOCKS // 2), True, False)
+        for a in (0, H):
+            product(GATE, plain1, gate_p1[:, a : a + H], a, a + H)
+        gate_tanh(plain1, gate_p1[:], 0, CH)
+        for u in (turned0, turned1):
+            kept[u] = quarter_tile("kept", u)
+        keep_res(turned0, 0, CH, res_t0)
+        for a in (0, H):
+            keep_res(turned1, a, a + H, res_t1[a])
+        add_turned(sum_t0, kept[turned0], range(BLOCKS), False, True)
+        empty(turned0, sum_t0)
+        add_turned(sum_t1, mixed[turned1], range(BLOCKS // 2, BLOCKS), False, False)
+        add_turned(sum_t1, kept[turned1], range(BLOCKS), False, True)
+        empty(turned1, sum_t1)
+
+        differences = keep.tile([P, 2 * CH], F32, name="differences", tag=f"picked01{H}")
         gated = keep.tile([P, 2 * CH], F32, name="gated")
-        diff(u2, 0, CH, held[:, 0:CH])
-        diff(u3, 0, CH, held[:, CH : 2 * CH])
-        gate(u2, 0, CH, gated[:, 0:CH])
-        d[u3, H] = held[:, CH + H : 2 * CH]
-        d[u3, 0] = held[:, CH : CH + H]
-        gate(u3, 0, H, gated[:, CH : CH + H])
-        finish(u2, 0, CH, 0)
-        gate(u3, H, CH, gated[:, CH + H : 2 * CH])
-        finish(u3, 0, H, 0)
-        finish(u3, H, 384, H)
-        finish(u3, 384, CH, H)
+        d0, d1 = differences[:, 0:CH], differences[:, CH : 2 * CH]
+        e0, e1 = gated[:, 0:CH], gated[:, CH : 2 * CH]
+        difference(plain0, d0)
+        difference(plain1, d1)
+        gate(plain0, 0, CH, e0, d0)
+        gate(plain1, 0, H, e1, d1)
+        finish(plain0, 0, CH, e0)
+        gate(plain1, H, CH, e1, d1)
+        for a, b in ((0, H), (H, CH - P), (CH - P, CH)):
+            finish(plain1, a, b, e1)

@@ -33,6 +33,7 @@ def tile_picked_highway_gelu_p_kernel(tc, x_words, x_scales, res, w1, w2, offs, 
     nc = tc.nc
     with ExitStack() as ctx:
         keep = ctx.enter_context(tc.tile_pool(name="keep", bufs=1))
+        turns = ctx.enter_context(tc.tile_pool(name="turns", bufs=1))
         psum = ctx.enter_context(tc.psum_pool(name="psum", bufs=1))
 
         def block(b):
@@ -67,46 +68,58 @@ def tile_picked_highway_gelu_p_kernel(tc, x_words, x_scales, res, w1, w2, offs, 
             nc.sync.dma_start(out=rows[:], in_=res[block(m), :])
             res_rows.append(rows)
 
-        grouped, codes, scales = {}, {}, {}
+        codes, scales = {}, {}
         for i in (GATE, LAYER):
             codes[i] = keep.tile([P, N], U32, name=f"codes{i}", align_bytes=64)
-            scales[i] = keep.tile([P, N], U8, name=f"scales{i}", align_bytes=64)
-            for m in range(N // P):
-                grouped[i, m] = keep.tile([P, P * PACK], BF16, name=f"grouped{i}{m}", align_bytes=64)
-                nc.scalar.copy(
-                    out=grouped[i, m][:].rearrange("p (c r t) -> p c t r", r=RUN, t=PACK),
-                    in_=raw[i][:, :, block(m)].rearrange("p t (c r) -> p c t r", r=RUN),
-                )
+        scales[GATE] = keep.tile([P, N], U8, name="scales_gate", align_bytes=64)
+        half = P * PACK
+        grouped_gate = turns.tile([P, 2 * half], BF16, name="grouped_gate", offset=2048, align_bytes=64)
+        grouped_first = keep.tile([P, half], BF16, name="grouped_first", align_bytes=64)
 
-        def quantize(i):
-            for m in range(N // P):
-                nc.vector.quantize_mx(
-                    out=codes[i][:, block(m)].bitcast(FP8X4), scales=scales[i][:, block(m)], in_=grouped[i, m][:]
-                )
+        def group_on_scalar(dst, i, m):
+            nc.scalar.copy(
+                out=dst.rearrange("p (c r t) -> p c t r", r=RUN, t=PACK),
+                in_=raw[i][:, :, block(m)].rearrange("p t (c r) -> p c t r", r=RUN),
+            )
+
+        def group_on_gpsimd(dst, i, m):
+            nc.gpsimd.tensor_scalar(
+                dst.rearrange("p (c t) -> p c t", t=PACK),
+                raw[i][:, :, block(m)].rearrange("p t c -> p c t"),
+                1.0,
+                0.0,
+                ALU.mult,
+                ALU.add,
+            )
 
         def entries(a, b):
             return offsets[:, a // PER_COL : b // PER_COL]
 
-        def pick_words(a, b, tag):
-            picked_words = keep.tile([P, b - a], U16, name=f"words{a}", tag=tag, align_bytes=64)
-            nc.vector.tensor_copy(picked_words[:], word_table[:].indirect(entries(a, b)))
-            return picked_words
-
-        words0 = pick_words(0, CH, "words_first")
+        group_on_scalar(grouped_gate[:, 0:half], GATE, 0)
+        group_on_gpsimd(grouped_gate[:, half : 2 * half], GATE, 1)
+        group_on_scalar(grouped_first[:], LAYER, 0)
+        words0 = keep.tile([P, CH], U16, name="words0", align_bytes=64)
+        nc.vector.tensor_copy(words0[:], word_table[:].indirect(entries(0, CH)))
         bytes0 = keep.tile([P, CH], U8, name="bytes0", align_bytes=64)
         nc.vector.tensor_copy(bytes0[:], scale_table[:].indirect(entries(0, CH)))
-        words1 = [pick_words(CH, CH + H, "words_second")]
-        quantize(GATE)
-        words1.append(pick_words(CH + H, S, f"raw{GATE}"))
-        quantize(LAYER)
-        bytes1 = keep.tile([P, CH], U8, name="bytes1", tag=f"raw{LAYER}", align_bytes=64)
+        nc.vector.quantize_mx(out=codes[GATE][:].bitcast(FP8X4), scales=scales[GATE][:], in_=grouped_gate[:])
+        grouped_second = turns.tile([P, half], BF16, name="grouped_second", offset=2048, align_bytes=64)
+        group_on_gpsimd(grouped_second[:], LAYER, 1)
+        words1 = turns.tile([P, CH], U16, name="words1", offset=3328, align_bytes=64)
+        nc.vector.tensor_copy(words1[:], word_table[:].indirect(entries(CH, S)))
+        scales[LAYER] = turns.tile([P, N], U8, name="scales_layer", offset=3072, align_bytes=64)
+        for m, src in ((0, grouped_first), (1, grouped_second)):
+            nc.vector.quantize_mx(
+                out=codes[LAYER][:, block(m)].bitcast(FP8X4), scales=scales[LAYER][:, block(m)], in_=src[:]
+            )
+        bytes1 = turns.tile([P, CH], U8, name="bytes1", offset=2560, align_bytes=64)
         for a in (0, H):
             nc.vector.tensor_copy(bytes1[:, a : a + H], scale_table[:].indirect(entries(CH + a, CH + a + H)))
 
         def tokens(c, a, b):
             if c == 0:
                 return words0[:, a:b].bitcast(FP4X4), bytes0[:, a:b]
-            return words1[a // H][:, a % H : a % H + b - a].bitcast(FP4X4), bytes1[:, a:b]
+            return words1[:, a:b].bitcast(FP4X4), bytes1[:, a:b]
 
         y, th, rest, mixed, picked, kept = {}, {}, {}, {}, {}, {}
 
@@ -148,10 +161,10 @@ def tile_picked_highway_gelu_p_kernel(tc, x_words, x_scales, res, w1, w2, offs, 
                 y[u] = quarter_tile("y", u)
             nc.scalar.activation(y[u][:, a:b], src, ACT.Gelu_apprx_tanh)
 
-        def gate_tanh(u, src, a, b):
+        def gate_tanh(u, src, a, b, scale=-0.5):
             if u not in th:
                 th[u] = quarter_tile("th", u)
-            nc.scalar.activation(th[u][:, a:b], src, ACT.Tanh, scale=-0.5)
+            nc.scalar.activation(th[u][:, a:b], src, ACT.Tanh, scale=scale)
 
         def mix(u, a, b):
             if u not in mixed:
@@ -183,11 +196,11 @@ def tile_picked_highway_gelu_p_kernel(tc, x_words, x_scales, res, w1, w2, offs, 
 
         def store(u, a, b, piece, queue):
             m, c = u
-            queue.dma_start(out=out[block(m), c * CH + a : c * CH + b], in_=piece[:])
+            queue.dma_start(out=out[block(m), c * CH + a : c * CH + b], in_=piece)
 
         def empty(u, src):
-            piece = quarter_tile("result", u)
-            nc.scalar.activation(piece[:], src[:], ACT.Copy, scale=0.5)
+            piece = results[:, u[1] * CH : (u[1] + 1) * CH]
+            nc.scalar.activation(piece, src[:], ACT.Copy, scale=0.5)
             store(u, 0, CH, piece, nc.scalar)
 
         def difference(u, dst):
@@ -200,76 +213,97 @@ def tile_picked_highway_gelu_p_kernel(tc, x_words, x_scales, res, w1, w2, offs, 
         def finish(u, a, b, src):
             piece = keep.tile([P, b - a], F32, name=f"result{u[0]}{u[1]}{a}")
             nc.vector.scalar_tensor_tensor(piece[:], src[:, a:b], 0.5, y[u][:, a:b], ALU.mult, ALU.add)
-            store(u, a, b, piece, nc.sync)
+            store(u, a, b, piece[:], nc.sync)
 
         turned0, turned1, plain0, plain1 = (0, 0), (0, 1), (1, 0), (1, 1)
 
-        gate_t0, gate_p0, layer_t0 = bank("A"), bank("B"), bank("C")
+        gate_t0, layer_t0, gate_p0, layer_p0 = bank("A"), bank("C"), bank("B"), bank("F")
         product_turned(GATE, turned0, gate_t0[:], 0, CH)
         product(GATE, plain0, gate_p0[:], 0, CH)
         product_turned(LAYER, turned0, layer_t0[:], 0, CH)
+        product(LAYER, plain0, layer_p0[:], 0, CH)
         both_t1 = {0: bank("D"), H: bank("E")}
         for a in (0, H):
             product_turned(GATE, turned1, both_t1[a][:, 0:H], a, a + H)
             product_turned(LAYER, turned1, both_t1[a][:, H:CH], a, a + H)
-        layer_p0 = bank("F")
-        product(LAYER, plain0, layer_p0[:], 0, CH)
+        layer_p1, gate_p1 = bank("G"), bank("H")
+        for a in (0, H):
+            product(LAYER, plain1, layer_p1[:, a : a + H], a, a + H)
+        for a in (0, H):
+            product(GATE, plain1, gate_p1[:, a : a + H], a, a + H)
 
         gate_tanh(turned0, gate_t0[:], 0, CH)
-        rest[turned0] = keep.tile([P, CH], F32, name="rest00", tag=f"grouped{LAYER}1", align_bytes=64)
+        rest[turned0] = turns.tile([P, CH], F32, name="rest00", offset=512, align_bytes=64)
         nc.gpsimd.tensor_scalar(rest[turned0][:], th[turned0][:], -1.0, 1.0, ALU.mult, ALU.add)
         gate_tanh(plain0, gate_p0[:], 0, CH)
         layer(turned0, layer_t0[:], 0, CH)
         mix(turned0, 0, CH)
-        for a in (0, H):
-            gate_tanh(turned1, both_t1[a][:, 0:H], a, a + H)
-            if a == 0:
-                rest[turned1] = quarter_tile("rest", turned1)
-            nc.scalar.activation(
-                rest[turned1][:, a : a + H], th[turned1][:, a : a + H], ACT.Identity, bias=1.0, scale=-1.0
-            )
-            layer(turned1, both_t1[a][:, H:CH], a, a + H)
-            mix(turned1, a, a + H)
         layer(plain0, layer_p0[:], 0, CH)
-
-        pick_res(turned0, 0, CH)
-        pick_res(turned1, 0, H)
-        pick_res(turned1, H, CH)
-        res_t0 = bank("A")
-        turn_res(turned0, 0, CH, res_t0)
-        layer_p1, gate_p1 = bank("G"), bank("H")
         for a in (0, H):
-            product(LAYER, plain1, layer_p1[:, a : a + H], a, a + H)
+            gate_tanh(turned1, both_t1[a][:, 0:H], a, a + H, 0.5)
+            layer(turned1, both_t1[a][:, H:CH], a, a + H)
+        rest[turned1] = th[turned1]
+        mix(turned1, 0, CH)
         layer(plain1, layer_p1[:], 0, CH)
-        res_t1 = {0: bank("B")}
-        turn_res(turned1, 0, H, res_t1[0])
+        gate_tanh(plain1, gate_p1[:], 0, CH)
+
+        picked[turned1, 0] = quarter_tile("picked", turned1)
+        nc.vector.tensor_scalar(
+            picked[turned1, 0][:], res_rows[0][:].indirect(entries(CH, S)), -1.0, 0.0, ALU.mult, ALU.add
+        )
+        pick_res(turned0, 0, H)
+        pick_res(turned0, H, CH)
+        res_t1 = bank("A")
+        turn_res(turned1, 0, CH, res_t1)
         sum_t0 = bank("C")
         add_turned(sum_t0, mixed[turned0], range(BLOCKS), True, False)
-        res_t1[H] = bank("E")
-        turn_res(turned1, H, CH, res_t1[H])
+        res_t0 = {0: bank("B"), H: bank("E")}
+        turn_res(turned0, 0, H, res_t0[0])
         sum_t1 = bank("D")
-        add_turned(sum_t1, mixed[turned1], range(BLOCKS // 2), True, False)
-        for a in (0, H):
-            product(GATE, plain1, gate_p1[:, a : a + H], a, a + H)
-        gate_tanh(plain1, gate_p1[:], 0, CH)
+        add_turned(sum_t1, y[turned1], range(BLOCKS), True, False)
+        turn_res(turned0, H, CH, res_t0[H])
+
+        def pick_on_scalar(u, a, b):
+            m, c = u
+            nc.scalar.activation(
+                picked[u][:, a:b], res_rows[m][:].indirect(entries(c * CH + a, c * CH + b)), ACT.Copy
+            )
+
+        for u in (plain0, plain1):
+            picked[u] = quarter_tile("picked", u)
+        pick_on_scalar(plain0, 0, H)
+        pick_on_scalar(plain0, H, CH)
+        pick_on_scalar(plain1, 0, H)
+
         for u in (turned0, turned1):
             kept[u] = quarter_tile("kept", u)
-        keep_res(turned0, 0, CH, res_t0)
+        nc.vector.scalar_tensor_tensor(kept[turned1][:], th[turned1][:], 1.0, res_t1[:], ALU.subtract, ALU.mult)
         for a in (0, H):
-            keep_res(turned1, a, a + H, res_t1[a])
-        add_turned(sum_t0, kept[turned0], range(BLOCKS), False, True)
-        empty(turned0, sum_t0)
-        add_turned(sum_t1, mixed[turned1], range(BLOCKS // 2, BLOCKS), False, False)
-        add_turned(sum_t1, kept[turned1], range(BLOCKS), False, True)
-        empty(turned1, sum_t1)
+            keep_res(turned0, a, a + H, res_t0[a])
 
-        differences = keep.tile([P, 2 * CH], F32, name="differences", tag=f"picked01{H}")
+        differences = keep.tile([P, 2 * CH], F32, name="differences", tag=f"picked00{H}")
         gated = keep.tile([P, 2 * CH], F32, name="gated")
         d0, d1 = differences[:, 0:CH], differences[:, CH : 2 * CH]
         e0, e1 = gated[:, 0:CH], gated[:, CH : 2 * CH]
-        difference(plain0, d0)
-        difference(plain1, d1)
-        gate(plain0, 0, CH, e0, d0)
+        nc.vector.tensor_tensor(
+            d1[:, H:CH], res_rows[1][:].indirect(entries(CH + H, S)), y[plain1][:, H:CH], ALU.subtract
+        )
+
+        results = keep.tile([P, S], F32, name="results", tag="res_rows1")
+        add_turned(sum_t1, kept[turned1], range(BLOCKS), False, False)
+        add_turned(sum_t0, kept[turned0], range(BLOCKS), False, True)
+        empty(turned0, sum_t0)
+        add_turned(sum_t1, mixed[turned1], range(BLOCKS), False, True)
+        empty(turned1, sum_t1)
+
+        def subtract(u, a, b, dst):
+            nc.vector.tensor_tensor(dst[:, a:b], picked[u][:, a:b], y[u][:, a:b], ALU.subtract)
+
+        subtract(plain0, 0, H, d0)
+        subtract(plain0, H, CH, d0)
+        gate(plain0, 0, H, e0, d0)
+        subtract(plain1, 0, H, d1)
+        gate(plain0, H, CH, e0, d0)
         gate(plain1, 0, H, e1, d1)
         finish(plain0, 0, CH, e0)
         gate(plain1, H, CH, e1, d1)

@@ -127,7 +127,7 @@ def tile_picked_highway_gelu_p_kernel(tc, x_words, x_scales, res, w1, w2, offs, 
             return psum.tile([P, CH], F32, name="bank", tag=tag)
 
         def quarter_tile(kind, u):
-            return keep.tile([P, CH], F32, name=f"{kind}{u[0]}{u[1]}")
+            return keep.tile([P, CH], F32, name=f"{kind}{u[0]}{u[1]}", tag=f"{kind}{u[0]}{u[1]}")
 
         def product(i, u, acc, a, b):
             m, c = u
@@ -210,8 +210,9 @@ def tile_picked_highway_gelu_p_kernel(tc, x_words, x_scales, res, w1, w2, offs, 
         def gate(u, a, b, dst, src):
             nc.vector.scalar_tensor_tensor(dst[:, a:b], th[u][:, a:b], 1.0, src[:, a:b], ALU.add, ALU.mult)
 
-        def finish(u, a, b, src):
-            piece = keep.tile([P, b - a], F32, name=f"result{u[0]}{u[1]}{a}")
+        def finish(u, a, b, src, tag=None):
+            name = f"result{u[0]}{u[1]}{a}"
+            piece = keep.tile([P, b - a], F32, name=name, tag=tag or name)
             nc.vector.scalar_tensor_tensor(piece[:], src[:, a:b], 0.5, y[u][:, a:b], ALU.mult, ALU.add)
             store(u, a, b, piece[:], nc.sync)
 
@@ -269,11 +270,8 @@ def tile_picked_highway_gelu_p_kernel(tc, x_words, x_scales, res, w1, w2, offs, 
                 picked[u][:, a:b], res_rows[m][:].indirect(entries(c * CH + a, c * CH + b)), ACT.Copy
             )
 
-        for u in (plain0, plain1):
-            picked[u] = quarter_tile("picked", u)
-        pick_on_scalar(plain0, 0, H)
-        pick_on_scalar(plain0, H, CH)
-        pick_on_scalar(plain1, 0, H)
+        picked[plain1] = quarter_tile("picked", plain1)
+        pick_on_scalar(plain1, 0, CH)
 
         for u in (turned0, turned1):
             kept[u] = quarter_tile("kept", u)
@@ -281,31 +279,27 @@ def tile_picked_highway_gelu_p_kernel(tc, x_words, x_scales, res, w1, w2, offs, 
         for a in (0, H):
             keep_res(turned0, a, a + H, res_t0[a])
 
+        results = keep.tile([P, S], F32, name="results")
+        add_turned(sum_t1, kept[turned1], range(BLOCKS), False, False)
+        add_turned(sum_t1, mixed[turned1], range(BLOCKS), False, True)
+        empty(turned1, sum_t1)
+        add_turned(sum_t0, kept[turned0], range(BLOCKS), False, True)
+        empty(turned0, sum_t0)
+
         differences = keep.tile([P, 2 * CH], F32, name="differences", tag=f"picked00{H}")
         gated = keep.tile([P, 2 * CH], F32, name="gated")
         d0, d1 = differences[:, 0:CH], differences[:, CH : 2 * CH]
         e0, e1 = gated[:, 0:CH], gated[:, CH : 2 * CH]
-        nc.vector.tensor_tensor(
-            d1[:, H:CH], res_rows[1][:].indirect(entries(CH + H, S)), y[plain1][:, H:CH], ALU.subtract
-        )
-
-        results = keep.tile([P, S], F32, name="results", tag="res_rows1")
-        add_turned(sum_t1, kept[turned1], range(BLOCKS), False, False)
-        add_turned(sum_t0, kept[turned0], range(BLOCKS), False, True)
-        empty(turned0, sum_t0)
-        add_turned(sum_t1, mixed[turned1], range(BLOCKS), False, True)
-        empty(turned1, sum_t1)
 
         def subtract(u, a, b, dst):
             nc.vector.tensor_tensor(dst[:, a:b], picked[u][:, a:b], y[u][:, a:b], ALU.subtract)
 
-        subtract(plain0, 0, H, d0)
-        subtract(plain0, H, CH, d0)
-        gate(plain0, 0, H, e0, d0)
+        difference(plain0, d0)
         subtract(plain1, 0, H, d1)
-        gate(plain0, H, CH, e0, d0)
-        gate(plain1, 0, H, e1, d1)
+        gate(plain0, 0, CH, e0, d0)
+        subtract(plain1, H, CH, d1)
         finish(plain0, 0, CH, e0)
-        gate(plain1, H, CH, e1, d1)
+        for a in (0, H):
+            gate(plain1, a, a + H, e1, d1)
         for a, b in ((0, H), (H, CH - P), (CH - P, CH)):
             finish(plain1, a, b, e1)

@@ -33,7 +33,6 @@ def tile_picked_highway_gelu_p_kernel(tc, x_words, x_scales, res, w1, w2, offs, 
     nc = tc.nc
     with ExitStack() as ctx:
         keep = ctx.enter_context(tc.tile_pool(name="keep", bufs=1))
-        turns = ctx.enter_context(tc.tile_pool(name="turns", bufs=1))
         psum = ctx.enter_context(tc.psum_pool(name="psum", bufs=1))
 
         def block(b):
@@ -68,58 +67,46 @@ def tile_picked_highway_gelu_p_kernel(tc, x_words, x_scales, res, w1, w2, offs, 
             nc.sync.dma_start(out=rows[:], in_=res[block(m), :])
             res_rows.append(rows)
 
-        codes, scales = {}, {}
+        grouped, codes, scales = {}, {}, {}
         for i in (GATE, LAYER):
             codes[i] = keep.tile([P, N], U32, name=f"codes{i}", align_bytes=64)
-        scales[GATE] = keep.tile([P, N], U8, name="scales_gate", align_bytes=64)
-        half = P * PACK
-        grouped_gate = turns.tile([P, 2 * half], BF16, name="grouped_gate", offset=2048, align_bytes=64)
-        grouped_first = keep.tile([P, half], BF16, name="grouped_first", align_bytes=64)
+            scales[i] = keep.tile([P, N], U8, name=f"scales{i}", align_bytes=64)
+            for m in range(N // P):
+                grouped[i, m] = keep.tile([P, P * PACK], BF16, name=f"grouped{i}{m}", align_bytes=64)
+                nc.scalar.copy(
+                    out=grouped[i, m][:].rearrange("p (c r t) -> p c t r", r=RUN, t=PACK),
+                    in_=raw[i][:, :, block(m)].rearrange("p t (c r) -> p c t r", r=RUN),
+                )
 
-        def group_on_scalar(dst, i, m):
-            nc.scalar.copy(
-                out=dst.rearrange("p (c r t) -> p c t r", r=RUN, t=PACK),
-                in_=raw[i][:, :, block(m)].rearrange("p t (c r) -> p c t r", r=RUN),
-            )
-
-        def group_on_gpsimd(dst, i, m):
-            nc.gpsimd.tensor_scalar(
-                dst.rearrange("p (c t) -> p c t", t=PACK),
-                raw[i][:, :, block(m)].rearrange("p t c -> p c t"),
-                1.0,
-                0.0,
-                ALU.mult,
-                ALU.add,
-            )
+        def quantize(i):
+            for m in range(N // P):
+                nc.vector.quantize_mx(
+                    out=codes[i][:, block(m)].bitcast(FP8X4), scales=scales[i][:, block(m)], in_=grouped[i, m][:]
+                )
 
         def entries(a, b):
             return offsets[:, a // PER_COL : b // PER_COL]
 
-        group_on_scalar(grouped_gate[:, 0:half], GATE, 0)
-        group_on_gpsimd(grouped_gate[:, half : 2 * half], GATE, 1)
-        group_on_scalar(grouped_first[:], LAYER, 0)
-        words0 = keep.tile([P, CH], U16, name="words0", align_bytes=64)
-        nc.vector.tensor_copy(words0[:], word_table[:].indirect(entries(0, CH)))
+        def pick_words(a, b, tag):
+            picked_words = keep.tile([P, b - a], U16, name=f"words{a}", tag=tag, align_bytes=64)
+            nc.vector.tensor_copy(picked_words[:], word_table[:].indirect(entries(a, b)))
+            return picked_words
+
+        words0 = pick_words(0, CH, "words_first")
         bytes0 = keep.tile([P, CH], U8, name="bytes0", align_bytes=64)
         nc.vector.tensor_copy(bytes0[:], scale_table[:].indirect(entries(0, CH)))
-        nc.vector.quantize_mx(out=codes[GATE][:].bitcast(FP8X4), scales=scales[GATE][:], in_=grouped_gate[:])
-        grouped_second = turns.tile([P, half], BF16, name="grouped_second", offset=2048, align_bytes=64)
-        group_on_gpsimd(grouped_second[:], LAYER, 1)
-        words1 = turns.tile([P, CH], U16, name="words1", offset=3328, align_bytes=64)
-        nc.vector.tensor_copy(words1[:], word_table[:].indirect(entries(CH, S)))
-        scales[LAYER] = turns.tile([P, N], U8, name="scales_layer", offset=3072, align_bytes=64)
-        for m, src in ((0, grouped_first), (1, grouped_second)):
-            nc.vector.quantize_mx(
-                out=codes[LAYER][:, block(m)].bitcast(FP8X4), scales=scales[LAYER][:, block(m)], in_=src[:]
-            )
-        bytes1 = turns.tile([P, CH], U8, name="bytes1", offset=2560, align_bytes=64)
+        words1 = [pick_words(CH, CH + H, "words_second")]
+        quantize(GATE)
+        words1.append(pick_words(CH + H, S, f"raw{GATE}"))
+        quantize(LAYER)
+        bytes1 = keep.tile([P, CH], U8, name="bytes1", tag=f"raw{LAYER}", align_bytes=64)
         for a in (0, H):
             nc.vector.tensor_copy(bytes1[:, a : a + H], scale_table[:].indirect(entries(CH + a, CH + a + H)))
 
         def tokens(c, a, b):
             if c == 0:
                 return words0[:, a:b].bitcast(FP4X4), bytes0[:, a:b]
-            return words1[:, a:b].bitcast(FP4X4), bytes1[:, a:b]
+            return words1[a // H][:, a % H : a % H + b - a].bitcast(FP4X4), bytes1[:, a:b]
 
         y, th, rest, mixed, picked, kept = {}, {}, {}, {}, {}, {}
 
@@ -203,16 +190,16 @@ def tile_picked_highway_gelu_p_kernel(tc, x_words, x_scales, res, w1, w2, offs, 
             nc.scalar.activation(piece, src[:], ACT.Copy, scale=0.5)
             store(u, 0, CH, piece, nc.scalar)
 
-        def difference(u, dst):
+        def difference(u, a, b, dst):
             m, c = u
-            nc.vector.tensor_tensor(dst, res_rows[m][:].indirect(entries(c * CH, (c + 1) * CH)), y[u][:], ALU.subtract)
+            looked_up = res_rows[m][:].indirect(entries(c * CH + a, c * CH + b))
+            nc.vector.tensor_tensor(dst[:, a:b], looked_up, y[u][:, a:b], ALU.subtract)
 
         def gate(u, a, b, dst, src):
             nc.vector.scalar_tensor_tensor(dst[:, a:b], th[u][:, a:b], 1.0, src[:, a:b], ALU.add, ALU.mult)
 
-        def finish(u, a, b, src, tag=None):
-            name = f"result{u[0]}{u[1]}{a}"
-            piece = keep.tile([P, b - a], F32, name=name, tag=tag or name)
+        def finish(u, a, b, src):
+            piece = keep.tile([P, b - a], F32, name=f"result{u[0]}{u[1]}{a}")
             nc.vector.scalar_tensor_tensor(piece[:], src[:, a:b], 0.5, y[u][:, a:b], ALU.mult, ALU.add)
             store(u, a, b, piece[:], nc.sync)
 
@@ -222,11 +209,11 @@ def tile_picked_highway_gelu_p_kernel(tc, x_words, x_scales, res, w1, w2, offs, 
         product_turned(GATE, turned0, gate_t0[:], 0, CH)
         product(GATE, plain0, gate_p0[:], 0, CH)
         product_turned(LAYER, turned0, layer_t0[:], 0, CH)
-        product(LAYER, plain0, layer_p0[:], 0, CH)
         both_t1 = {0: bank("D"), H: bank("E")}
         for a in (0, H):
             product_turned(GATE, turned1, both_t1[a][:, 0:H], a, a + H)
             product_turned(LAYER, turned1, both_t1[a][:, H:CH], a, a + H)
+        product(LAYER, plain0, layer_p0[:], 0, CH)
         layer_p1, gate_p1 = bank("G"), bank("H")
         for a in (0, H):
             product(LAYER, plain1, layer_p1[:, a : a + H], a, a + H)
@@ -234,19 +221,18 @@ def tile_picked_highway_gelu_p_kernel(tc, x_words, x_scales, res, w1, w2, offs, 
             product(GATE, plain1, gate_p1[:, a : a + H], a, a + H)
 
         gate_tanh(turned0, gate_t0[:], 0, CH)
-        rest[turned0] = turns.tile([P, CH], F32, name="rest00", offset=512, align_bytes=64)
+        rest[turned0] = keep.tile([P, CH], F32, name="rest00", tag=f"grouped{LAYER}1", align_bytes=64)
         nc.gpsimd.tensor_scalar(rest[turned0][:], th[turned0][:], -1.0, 1.0, ALU.mult, ALU.add)
         gate_tanh(plain0, gate_p0[:], 0, CH)
         layer(turned0, layer_t0[:], 0, CH)
         mix(turned0, 0, CH)
-        layer(plain0, layer_p0[:], 0, CH)
         for a in (0, H):
             gate_tanh(turned1, both_t1[a][:, 0:H], a, a + H, 0.5)
             layer(turned1, both_t1[a][:, H:CH], a, a + H)
         rest[turned1] = th[turned1]
         mix(turned1, 0, CH)
+        layer(plain0, layer_p0[:], 0, CH)
         layer(plain1, layer_p1[:], 0, CH)
-        gate_tanh(plain1, gate_p1[:], 0, CH)
 
         picked[turned1, 0] = quarter_tile("picked", turned1)
         nc.vector.tensor_scalar(
@@ -258,11 +244,11 @@ def tile_picked_highway_gelu_p_kernel(tc, x_words, x_scales, res, w1, w2, offs, 
         turn_res(turned1, 0, CH, res_t1)
         sum_t0 = bank("C")
         add_turned(sum_t0, mixed[turned0], range(BLOCKS), True, False)
-        res_t0 = {0: bank("B"), H: bank("E")}
+        res_t0 = {0: bank("B"), H: bank("D")}
         turn_res(turned0, 0, H, res_t0[0])
-        sum_t1 = bank("D")
-        add_turned(sum_t1, y[turned1], range(BLOCKS), True, False)
         turn_res(turned0, H, CH, res_t0[H])
+        sum_t1 = bank("E")
+        add_turned(sum_t1, y[turned1], range(BLOCKS), True, False)
 
         def pick_on_scalar(u, a, b):
             m, c = u
@@ -272,6 +258,7 @@ def tile_picked_highway_gelu_p_kernel(tc, x_words, x_scales, res, w1, w2, offs, 
 
         picked[plain1] = quarter_tile("picked", plain1)
         pick_on_scalar(plain1, 0, CH)
+        gate_tanh(plain1, gate_p1[:], 0, CH)
 
         for u in (turned0, turned1):
             kept[u] = quarter_tile("kept", u)
@@ -294,9 +281,11 @@ def tile_picked_highway_gelu_p_kernel(tc, x_words, x_scales, res, w1, w2, offs, 
         def subtract(u, a, b, dst):
             nc.vector.tensor_tensor(dst[:, a:b], picked[u][:, a:b], y[u][:, a:b], ALU.subtract)
 
-        difference(plain0, d0)
+        for a in (0, H):
+            difference(plain0, a, a + H, d0)
+        gate(plain0, 0, H, e0, d0)
         subtract(plain1, 0, H, d1)
-        gate(plain0, 0, CH, e0, d0)
+        gate(plain0, H, CH, e0, d0)
         subtract(plain1, H, CH, d1)
         finish(plain0, 0, CH, e0)
         for a in (0, H):

@@ -258,7 +258,6 @@ def tile_picked_highway_gelu_p_kernel(tc, x_words, x_scales, res, w1, w2, offs, 
 
         picked[plain1] = quarter_tile("picked", plain1)
         pick_on_scalar(plain1, 0, CH)
-        gate_tanh(plain1, gate_p1[:], 0, CH)
 
         for u in (turned0, turned1):
             kept[u] = quarter_tile("kept", u)
@@ -269,6 +268,8 @@ def tile_picked_highway_gelu_p_kernel(tc, x_words, x_scales, res, w1, w2, offs, 
         results = keep.tile([P, S], F32, name="results")
         add_turned(sum_t1, kept[turned1], range(BLOCKS), False, False)
         add_turned(sum_t1, mixed[turned1], range(BLOCKS), False, True)
+        th[plain1] = keep.tile([P, CH], F32, name="th11", tag="kept01")
+        gate_tanh(plain1, gate_p1[:], 0, CH)
         empty(turned1, sum_t1)
         add_turned(sum_t0, kept[turned0], range(BLOCKS), False, True)
         empty(turned0, sum_t0)

@@ -68,9 +68,10 @@ def tile_picked_highway_gelu_p_kernel(tc, x_words, x_scales, res, w1, w2, offs, 
             res_rows.append(rows)
 
         grouped, codes, scales = {}, {}, {}
+        for m in range(N // P):
+            codes[m] = keep.tile([P, 2 * P], U32, name=f"codes{m}", align_bytes=64)
+            scales[m] = keep.tile([P, 2 * P], U8, name=f"scales{m}", align_bytes=64)
         for i in (GATE, LAYER):
-            codes[i] = keep.tile([P, N], U32, name=f"codes{i}", align_bytes=64)
-            scales[i] = keep.tile([P, N], U8, name=f"scales{i}", align_bytes=64)
             for m in range(N // P):
                 grouped[i, m] = keep.tile([P, P * PACK], BF16, name=f"grouped{i}{m}", align_bytes=64)
                 nc.scalar.copy(
@@ -81,7 +82,7 @@ def tile_picked_highway_gelu_p_kernel(tc, x_words, x_scales, res, w1, w2, offs, 
         def quantize(i):
             for m in range(N // P):
                 nc.vector.quantize_mx(
-                    out=codes[i][:, block(m)].bitcast(FP8X4), scales=scales[i][:, block(m)], in_=grouped[i, m][:]
+                    out=codes[m][:, block(i)].bitcast(FP8X4), scales=scales[m][:, block(i)], in_=grouped[i, m][:]
                 )
 
         def entries(a, b):
@@ -121,8 +122,8 @@ def tile_picked_highway_gelu_p_kernel(tc, x_words, x_scales, res, w1, w2, offs, 
             words, scale_bytes = tokens(c, a, b)
             nc.tensor.matmul_mx(
                 out=acc,
-                lhsT=codes[i][:, block(m)].bitcast(FP8X4),
-                lhsT_scale=scales[i][:, block(m)],
+                lhsT=codes[m][:, block(i)].bitcast(FP8X4),
+                lhsT_scale=scales[m][:, block(i)],
                 rhs=words,
                 rhs_scale=scale_bytes,
                 start=True,
@@ -137,8 +138,8 @@ def tile_picked_highway_gelu_p_kernel(tc, x_words, x_scales, res, w1, w2, offs, 
                     out=acc[:, block(n)],
                     lhsT=words,
                     lhsT_scale=scale_bytes,
-                    rhs=codes[i][:, block(m)].bitcast(FP8X4),
-                    rhs_scale=scales[i][:, block(m)],
+                    rhs=codes[m][:, block(i)].bitcast(FP8X4),
+                    rhs_scale=scales[m][:, block(i)],
                     start=True,
                     stop=True,
                 )
@@ -211,8 +212,17 @@ def tile_picked_highway_gelu_p_kernel(tc, x_words, x_scales, res, w1, w2, offs, 
         product_turned(LAYER, turned0, layer_t0[:], 0, CH)
         both_t1 = {0: bank("D"), H: bank("E")}
         for a in (0, H):
-            product_turned(GATE, turned1, both_t1[a][:, 0:H], a, a + H)
-            product_turned(LAYER, turned1, both_t1[a][:, H:CH], a, a + H)
+            for n in range(H // P):
+                words, scale_bytes = tokens(1, a + n * P, a + (n + 1) * P)
+                nc.tensor.matmul_mx(
+                    out=both_t1[a][:, n * H : (n + 1) * H],
+                    lhsT=words,
+                    lhsT_scale=scale_bytes,
+                    rhs=codes[0][:].bitcast(FP8X4),
+                    rhs_scale=scales[0][:],
+                    start=True,
+                    stop=True,
+                )
         product(LAYER, plain0, layer_p0[:], 0, CH)
         layer_p1, gate_p1 = bank("G"), bank("H")
         for a in (0, H):
@@ -227,8 +237,12 @@ def tile_picked_highway_gelu_p_kernel(tc, x_words, x_scales, res, w1, w2, offs, 
         layer(turned0, layer_t0[:], 0, CH)
         mix(turned0, 0, CH)
         for a in (0, H):
-            gate_tanh(turned1, both_t1[a][:, 0:H], a, a + H, 0.5)
-            layer(turned1, both_t1[a][:, H:CH], a, a + H)
+            sides = both_t1[a][:].rearrange("p (n i f) -> p i n f", i=2, f=P)
+            for kind, store_of, i, func, scale in (("th", th, GATE, ACT.Tanh, 0.5), ("y", y, LAYER, ACT.Gelu_apprx_tanh, 1.0)):
+                if turned1 not in store_of:
+                    store_of[turned1] = quarter_tile(kind, turned1)
+                dst = store_of[turned1][:, a : a + H].rearrange("p (n f) -> p n f", f=P)
+                nc.scalar.activation(dst, sides[:, i], func, scale=scale)
         rest[turned1] = th[turned1]
         mix(turned1, 0, CH)
         layer(plain0, layer_p0[:], 0, CH)

@@ -296,14 +296,11 @@ def tile_picked_highway_gelu_p_kernel(tc, x_words, x_scales, res, w1, w2, offs, 
         def subtract(u, a, b, dst):
             nc.vector.tensor_tensor(dst[:, a:b], picked[u][:, a:b], y[u][:, a:b], ALU.subtract)
 
-        for a in (0, H):
-            difference(plain0, a, a + H, d0)
-        gate(plain0, 0, H, e0, d0)
-        subtract(plain1, 0, H, d1)
-        gate(plain0, H, CH, e0, d0)
-        subtract(plain1, H, CH, d1)
+        difference(plain0, 0, CH, d0)
+        subtract(plain1, 0, CH, d1)
+        gate(plain0, 0, CH, e0, d0)
+        gate(plain1, 0, H, e1, d1)
         finish(plain0, 0, CH, e0)
-        for a in (0, H):
-            gate(plain1, a, a + H, e1, d1)
+        gate(plain1, H, CH, e1, d1)
         for a, b in ((0, H), (H, CH - P), (CH - P, CH)):
             finish(plain1, a, b, e1)

@@ -1,7 +1,6 @@
 from contextlib import ExitStack
 
 import concourse.mybir as mybir
-from concourse.masks import make_identity
 
 K, T, S, N = 512, 2048, 1024, 256
 FLOPS = 2 * 2 * K * N * S
@@ -25,7 +24,6 @@ SCALE_ROWS = 4
 PER_COL = 16
 CH = 512
 H = CH // 2
-BLOCKS = CH // P
 LAYER, GATE = 0, 1
 
 
@@ -33,6 +31,7 @@ def tile_picked_highway_gelu_p_kernel(tc, x_words, x_scales, res, w1, w2, offs, 
     nc = tc.nc
     with ExitStack() as ctx:
         keep = ctx.enter_context(tc.tile_pool(name="keep", bufs=1))
+        shared = ctx.enter_context(tc.tile_pool(name="shared", bufs=1))
         psum = ctx.enter_context(tc.psum_pool(name="psum", bufs=1))
 
         def block(b):
@@ -54,26 +53,26 @@ def tile_picked_highway_gelu_p_kernel(tc, x_words, x_scales, res, w1, w2, offs, 
                 out=scale_table[QUADRANT * q : QUADRANT * q + SCALE_ROWS, :].bitcast(I32),
                 in_=x_scales[0, SCALE_ROWS * q : SCALE_ROWS * (q + 1), :].bitcast(I32),
             )
-        identity = keep.tile([P, P], F32, name="identity")
-        make_identity(nc, identity[:])
 
+        RAW_BYTES = PACK * N * 4
+        raw_at = {GATE: 0, LAYER: RAW_BYTES}
         raw = {}
-        for i, w in ((GATE, w2), (LAYER, w1)):
-            raw[i] = keep.tile([P, PACK, N], F32, name=f"raw{i}", align_bytes=64)
+        for i, w in ((LAYER, w1), (GATE, w2)):
+            raw[i] = shared.tile([P, PACK, N], F32, name=f"raw{i}", align_bytes=64, offset=raw_at[i])
             nc.sync.dma_start(out=raw[i][:], in_=w.rearrange("(p t) c -> p t c", t=PACK))
+        res_at = [2 * RAW_BYTES, 2 * RAW_BYTES + 4 * T]
         res_rows = []
         for m in range(N // P):
-            rows = keep.tile([P, T], F32, name=f"res_rows{m}")
+            rows = shared.tile([P, T], F32, name=f"res_rows{m}", align_bytes=64, offset=res_at[m])
             nc.sync.dma_start(out=rows[:], in_=res[block(m), :])
             res_rows.append(rows)
 
         grouped, codes, scales = {}, {}, {}
-        for m in range(N // P):
-            codes[m] = keep.tile([P, 2 * P], U32, name=f"codes{m}", align_bytes=64)
-            scales[m] = keep.tile([P, 2 * P], U8, name=f"scales{m}", align_bytes=64)
-        for i in (GATE, LAYER):
+        for i in (LAYER, GATE):
             for m in range(N // P):
                 grouped[i, m] = keep.tile([P, P * PACK], BF16, name=f"grouped{i}{m}", align_bytes=64)
+                codes[i, m] = keep.tile([P, P], U32, name=f"codes{i}{m}", align_bytes=64)
+                scales[i, m] = keep.tile([P, P], U8, name=f"scales{i}{m}", align_bytes=64)
                 nc.scalar.copy(
                     out=grouped[i, m][:].rearrange("p (c r t) -> p c t r", r=RUN, t=PACK),
                     in_=raw[i][:, :, block(m)].rearrange("p t (c r) -> p c t r", r=RUN),
@@ -81,226 +80,114 @@ def tile_picked_highway_gelu_p_kernel(tc, x_words, x_scales, res, w1, w2, offs, 
 
         def quantize(i):
             for m in range(N // P):
-                nc.vector.quantize_mx(
-                    out=codes[m][:, block(i)].bitcast(FP8X4), scales=scales[m][:, block(i)], in_=grouped[i, m][:]
-                )
+                nc.vector.quantize_mx(out=codes[i, m][:].bitcast(FP8X4), scales=scales[i, m][:], in_=grouped[i, m][:])
 
         def entries(a, b):
             return offsets[:, a // PER_COL : b // PER_COL]
 
-        def pick_words(a, b, tag):
-            picked_words = keep.tile([P, b - a], U16, name=f"words{a}", tag=tag, align_bytes=64)
-            nc.vector.tensor_copy(picked_words[:], word_table[:].indirect(entries(a, b)))
-            return picked_words
+        def gather(dst, table, a, b):
+            nc.vector.tensor_copy(dst, table[:].indirect(entries(a, b)))
 
-        words0 = pick_words(0, CH, "words_first")
+        words0 = keep.tile([P, CH], U16, name="words0", align_bytes=64)
+        gather(words0[:], word_table, 0, CH)
         bytes0 = keep.tile([P, CH], U8, name="bytes0", align_bytes=64)
-        nc.vector.tensor_copy(bytes0[:], scale_table[:].indirect(entries(0, CH)))
-        words1 = [pick_words(CH, CH + H, "words_second")]
-        quantize(GATE)
-        words1.append(pick_words(CH + H, S, f"raw{GATE}"))
+        gather(bytes0[:], scale_table, 0, CH)
+        words1 = [keep.tile([P, H], U16, name="words1a", align_bytes=64)]
+        gather(words1[0][:], word_table, CH, CH + H)
         quantize(LAYER)
-        bytes1 = keep.tile([P, CH], U8, name="bytes1", tag=f"raw{LAYER}", align_bytes=64)
+        words1.append(shared.tile([P, H], U16, name="words1b", align_bytes=64, offset=raw_at[LAYER]))
+        gather(words1[1][:], word_table, CH + H, S)
+        quantize(GATE)
+        bytes1 = shared.tile([P, CH], U8, name="bytes1", align_bytes=64, offset=raw_at[GATE])
         for a in (0, H):
-            nc.vector.tensor_copy(bytes1[:, a : a + H], scale_table[:].indirect(entries(CH + a, CH + a + H)))
+            gather(bytes1[:, a : a + H], scale_table, CH + a, CH + a + H)
 
-        def tokens(c, a, b):
-            if c == 0:
-                return words0[:, a:b].bitcast(FP4X4), bytes0[:, a:b]
-            return words1[a // H][:, a % H : a % H + b - a].bitcast(FP4X4), bytes1[:, a:b]
+        acc, y, th, picked, diff, gated, zero = {}, {}, {}, {}, {}, {}, {}
 
-        y, th, rest, mixed, picked, kept = {}, {}, {}, {}, {}, {}
+        def tile_of(kind, u, tag=None):
+            name = f"{kind}{u[0]}{u[1]}"
+            if (kind, u) in on_res:
+                m, slot = on_res[kind, u]
+                return shared.tile([P, CH], F32, name=name, align_bytes=64, offset=res_at[m] + 4 * CH * slot)
+            return keep.tile([P, CH], F32, name=name, tag=tag or name)
 
-        def bank(tag):
-            return psum.tile([P, CH], F32, name="bank", tag=tag)
-
-        def quarter_tile(kind, u):
-            return keep.tile([P, CH], F32, name=f"{kind}{u[0]}{u[1]}", tag=f"{kind}{u[0]}{u[1]}")
-
-        def product(i, u, acc, a, b):
+        def product(i, u):
             m, c = u
-            words, scale_bytes = tokens(c, a, b)
-            nc.tensor.matmul_mx(
-                out=acc,
-                lhsT=codes[m][:, block(i)].bitcast(FP8X4),
-                lhsT_scale=scales[m][:, block(i)],
-                rhs=words,
-                rhs_scale=scale_bytes,
-                start=True,
-                stop=True,
-            )
-
-        def product_turned(i, u, acc, a, b):
-            m, c = u
-            for n in range((b - a) // P):
-                words, scale_bytes = tokens(c, a + n * P, a + (n + 1) * P)
+            acc[i, u] = psum.tile([P, CH], F32, name=f"acc{i}{m}{c}")
+            pieces = [(0, CH, words0[:], bytes0[:])]
+            if c == 1:
+                pieces = [(a, a + H, words1[a // H][:], bytes1[:, a : a + H]) for a in (0, H)]
+            for a, b, words, scale_bytes in pieces:
                 nc.tensor.matmul_mx(
-                    out=acc[:, block(n)],
-                    lhsT=words,
-                    lhsT_scale=scale_bytes,
-                    rhs=codes[m][:, block(i)].bitcast(FP8X4),
-                    rhs_scale=scales[m][:, block(i)],
+                    out=acc[i, u][:, a:b],
+                    lhsT=codes[i, m][:].bitcast(FP8X4),
+                    lhsT_scale=scales[i, m][:],
+                    rhs=words.bitcast(FP4X4),
+                    rhs_scale=scale_bytes,
                     start=True,
                     stop=True,
                 )
 
-        def layer(u, src, a, b):
-            if u not in y:
-                y[u] = quarter_tile("y", u)
-            nc.scalar.activation(y[u][:, a:b], src, ACT.Gelu_apprx_tanh)
+        def layer(u, hold=None):
+            y[u] = tile_of("y", u)
+            if hold is None:
+                nc.scalar.activation(y[u][:], acc[LAYER, u][:], ACT.Gelu_apprx_tanh)
+            else:
+                nc.scalar.activation(y[u][:], acc[LAYER, u][:], ACT.Gelu_apprx_tanh, bias=zero[hold][:])
 
-        def gate_tanh(u, src, a, b, scale=-0.5):
-            if u not in th:
-                th[u] = quarter_tile("th", u)
-            nc.scalar.activation(th[u][:, a:b], src, ACT.Tanh, scale=scale)
+        def gate_tanh(u):
+            th[u] = tile_of("th", u)
+            nc.scalar.activation(th[u][:], acc[GATE, u][:], ACT.Tanh, scale=-0.5)
 
-        def mix(u, a, b):
-            if u not in mixed:
-                mixed[u] = quarter_tile("mixed", u)
-            nc.gpsimd.tensor_tensor(mixed[u][:, a:b], rest[u][:, a:b], y[u][:, a:b], ALU.mult)
-
-        def pick_res(u, a, b):
+        def looked_up(u, a, b):
             m, c = u
-            picked[u, a] = keep.tile([P, b - a], F32, name=f"picked{m}{c}{a}")
-            nc.vector.tensor_copy(picked[u, a][:], res_rows[m][:].indirect(entries(c * CH + a, c * CH + b)))
+            return res_rows[m][:].indirect(entries(c * CH + a, c * CH + b))
 
-        def turn_res(u, a, b, dst):
-            for n in range((b - a) // P):
-                nc.tensor.transpose(dst[:, block(n)], picked[u, a][:, block(n)], identity[:])
+        def pick(u, a=0, b=CH):
+            if u not in picked:
+                picked[u] = tile_of("picked", u)
+            nc.scalar.activation(picked[u][:, a:b], looked_up(u, a, b), ACT.Copy)
 
-        def keep_res(u, a, b, src):
-            nc.vector.scalar_tensor_tensor(kept[u][:, a:b], th[u][:, a:b], 1.0, src[:, 0 : b - a], ALU.add, ALU.mult)
+        def subtract(u, a=0, b=CH, fused=False):
+            if u not in diff:
+                diff[u] = tile_of("diff", u)
+            src = looked_up(u, a, b) if fused else picked[u][:, a:b]
+            nc.vector.tensor_tensor(diff[u][:, a:b], src, y[u][:, a:b], ALU.subtract)
 
-        def add_turned(dst, src, blocks, opens, closes):
-            for n in blocks:
-                nc.tensor.matmul(
-                    dst[:, block(n)],
-                    src[:, block(n)],
-                    identity[:],
-                    start=(opens and n == blocks[0]),
-                    stop=(closes and n == blocks[-1]),
-                    is_transpose=True,
-                )
+        def gate(u, a=0, b=CH):
+            if u not in gated:
+                gated[u] = tile_of("gated", u)
+            nc.vector.scalar_tensor_tensor(gated[u][:, a:b], th[u][:, a:b], 1.0, diff[u][:, a:b], ALU.add, ALU.mult)
 
-        def store(u, a, b, piece, queue):
+        def finish(u, a=0, b=CH, tag=None):
             m, c = u
-            queue.dma_start(out=out[block(m), c * CH + a : c * CH + b], in_=piece)
+            name = f"result{m}{c}{a}"
+            piece = keep.tile([P, b - a], F32, name=name, tag=tag or name)
+            nc.vector.scalar_tensor_tensor(piece[:], gated[u][:, a:b], 0.5, y[u][:, a:b], ALU.mult, ALU.add)
+            nc.sync.dma_start(out=out[block(m), c * CH + a : c * CH + b], in_=piece[:])
 
-        def empty(u, src):
-            piece = results[:, u[1] * CH : (u[1] + 1) * CH]
-            nc.scalar.activation(piece, src[:], ACT.Copy, scale=0.5)
-            store(u, 0, CH, piece, nc.scalar)
+        q0, q1, q2, q3 = (0, 0), (0, 1), (1, 0), (1, 1)
+        on_res = {("y", q3): (1, 0), ("th", q3): (1, 1)}
 
-        def difference(u, a, b, dst):
-            m, c = u
-            looked_up = res_rows[m][:].indirect(entries(c * CH + a, c * CH + b))
-            nc.vector.tensor_tensor(dst[:, a:b], looked_up, y[u][:, a:b], ALU.subtract)
+        for i, u in ((LAYER, q0), (LAYER, q2), (GATE, q0), (GATE, q2), (LAYER, q1), (GATE, q1), (LAYER, q3), (GATE, q3)):
+            product(i, u)
 
-        def gate(u, a, b, dst, src):
-            nc.vector.scalar_tensor_tensor(dst[:, a:b], th[u][:, a:b], 1.0, src[:, a:b], ALU.add, ALU.mult)
+        layer(q0)
+        layer(q2)
+        gate_tanh(q0)
+        pick(q1)
+        layer(q1)
+        gate_tanh(q1)
+        gate_tanh(q2)
+        pick(q2, H, CH)
+        pick(q3)
+        layer(q3)
+        gate_tanh(q3)
 
-        def finish(u, a, b, src):
-            piece = keep.tile([P, b - a], F32, name=f"result{u[0]}{u[1]}{a}")
-            nc.vector.scalar_tensor_tensor(piece[:], src[:, a:b], 0.5, y[u][:, a:b], ALU.mult, ALU.add)
-            store(u, a, b, piece[:], nc.sync)
-
-        turned0, turned1, plain0, plain1 = (0, 0), (0, 1), (1, 0), (1, 1)
-
-        gate_t0, layer_t0, gate_p0, layer_p0 = bank("A"), bank("C"), bank("B"), bank("F")
-        product_turned(GATE, turned0, gate_t0[:], 0, CH)
-        product(GATE, plain0, gate_p0[:], 0, CH)
-        product_turned(LAYER, turned0, layer_t0[:], 0, CH)
-        both_t1 = {0: bank("D"), H: bank("E")}
-        for a in (0, H):
-            for n in range(H // P):
-                words, scale_bytes = tokens(1, a + n * P, a + (n + 1) * P)
-                nc.tensor.matmul_mx(
-                    out=both_t1[a][:, n * H : (n + 1) * H],
-                    lhsT=words,
-                    lhsT_scale=scale_bytes,
-                    rhs=codes[0][:].bitcast(FP8X4),
-                    rhs_scale=scales[0][:],
-                    start=True,
-                    stop=True,
-                )
-        product(LAYER, plain0, layer_p0[:], 0, CH)
-        layer_p1, gate_p1 = bank("G"), bank("H")
-        for a in (0, H):
-            product(LAYER, plain1, layer_p1[:, a : a + H], a, a + H)
-        for a in (0, H):
-            product(GATE, plain1, gate_p1[:, a : a + H], a, a + H)
-
-        gate_tanh(turned0, gate_t0[:], 0, CH)
-        rest[turned0] = keep.tile([P, CH], F32, name="rest00", tag=f"grouped{LAYER}1", align_bytes=64)
-        nc.gpsimd.tensor_scalar(rest[turned0][:], th[turned0][:], -1.0, 1.0, ALU.mult, ALU.add)
-        gate_tanh(plain0, gate_p0[:], 0, CH)
-        layer(turned0, layer_t0[:], 0, CH)
-        mix(turned0, 0, CH)
-        for a in (0, H):
-            sides = both_t1[a][:].rearrange("p (n i f) -> p i n f", i=2, f=P)
-            for kind, store_of, i, func, scale in (("th", th, GATE, ACT.Tanh, 0.5), ("y", y, LAYER, ACT.Gelu_apprx_tanh, 1.0)):
-                if turned1 not in store_of:
-                    store_of[turned1] = quarter_tile(kind, turned1)
-                dst = store_of[turned1][:, a : a + H].rearrange("p (n f) -> p n f", f=P)
-                nc.scalar.activation(dst, sides[:, i], func, scale=scale)
-        rest[turned1] = th[turned1]
-        mix(turned1, 0, CH)
-        layer(plain0, layer_p0[:], 0, CH)
-        layer(plain1, layer_p1[:], 0, CH)
-
-        picked[turned1, 0] = quarter_tile("picked", turned1)
-        nc.vector.tensor_scalar(
-            picked[turned1, 0][:], res_rows[0][:].indirect(entries(CH, S)), -1.0, 0.0, ALU.mult, ALU.add
-        )
-        pick_res(turned0, 0, H)
-        pick_res(turned0, H, CH)
-        res_t1 = bank("A")
-        turn_res(turned1, 0, CH, res_t1)
-        sum_t0 = bank("C")
-        add_turned(sum_t0, mixed[turned0], range(BLOCKS), True, False)
-        res_t0 = {0: bank("B"), H: bank("D")}
-        turn_res(turned0, 0, H, res_t0[0])
-        turn_res(turned0, H, CH, res_t0[H])
-        sum_t1 = bank("E")
-        add_turned(sum_t1, y[turned1], range(BLOCKS), True, False)
-
-        def pick_on_scalar(u, a, b):
-            m, c = u
-            nc.scalar.activation(
-                picked[u][:, a:b], res_rows[m][:].indirect(entries(c * CH + a, c * CH + b)), ACT.Copy
-            )
-
-        picked[plain1] = quarter_tile("picked", plain1)
-        pick_on_scalar(plain1, 0, CH)
-
-        for u in (turned0, turned1):
-            kept[u] = quarter_tile("kept", u)
-        nc.vector.scalar_tensor_tensor(kept[turned1][:], th[turned1][:], 1.0, res_t1[:], ALU.subtract, ALU.mult)
-        for a in (0, H):
-            keep_res(turned0, a, a + H, res_t0[a])
-
-        results = keep.tile([P, S], F32, name="results")
-        add_turned(sum_t1, kept[turned1], range(BLOCKS), False, False)
-        add_turned(sum_t1, mixed[turned1], range(BLOCKS), False, True)
-        th[plain1] = keep.tile([P, CH], F32, name="th11", tag="kept01")
-        gate_tanh(plain1, gate_p1[:], 0, CH)
-        empty(turned1, sum_t1)
-        add_turned(sum_t0, kept[turned0], range(BLOCKS), False, True)
-        empty(turned0, sum_t0)
-
-        differences = keep.tile([P, 2 * CH], F32, name="differences", tag=f"picked00{H}")
-        gated = keep.tile([P, 2 * CH], F32, name="gated")
-        d0, d1 = differences[:, 0:CH], differences[:, CH : 2 * CH]
-        e0, e1 = gated[:, 0:CH], gated[:, CH : 2 * CH]
-
-        def subtract(u, a, b, dst):
-            nc.vector.tensor_tensor(dst[:, a:b], picked[u][:, a:b], y[u][:, a:b], ALU.subtract)
-
-        difference(plain0, 0, CH, d0)
-        subtract(plain1, 0, CH, d1)
-        gate(plain0, 0, CH, e0, d0)
-        gate(plain1, 0, H, e1, d1)
-        finish(plain0, 0, CH, e0)
-        gate(plain1, H, CH, e1, d1)
-        for a, b in ((0, H), (H, CH - P), (CH - P, CH)):
-            finish(plain1, a, b, e1)
+        for u in (q0, q1, q2, q3):
+            for a in (0, H):
+                subtract(u, a, a + H, fused=(u == q0 or (u == q2 and a == 0)))
+            for a in (0, H):
+                gate(u, a, a + H)
+            for a, b in ((0, H), (H, CH)) if u != q3 else ((0, H), (H, CH - P), (CH - P, CH)):
+                finish(u, a, b)

@@ -135,9 +135,12 @@ def tile_picked_highway_gelu_p_kernel(tc, x_words, x_scales, res, w1, w2, offs, 
             else:
                 nc.scalar.activation(y[u][:], acc[LAYER, u][:], ACT.Gelu_apprx_tanh, bias=zero[hold][:])
 
-        def gate_tanh(u):
+        def gate_tanh(u, hold=None):
             th[u] = tile_of("th", u)
-            nc.scalar.activation(th[u][:], acc[GATE, u][:], ACT.Tanh, scale=-0.5)
+            if hold is None:
+                nc.scalar.activation(th[u][:], acc[GATE, u][:], ACT.Tanh, scale=-0.5)
+            else:
+                nc.scalar.activation(th[u][:], acc[GATE, u][:], ACT.Tanh, scale=-0.5, bias=zero[hold][:])
 
         def looked_up(u, a, b):
             m, c = u
@@ -154,9 +157,9 @@ def tile_picked_highway_gelu_p_kernel(tc, x_words, x_scales, res, w1, w2, offs, 
             src = looked_up(u, a, b) if fused else picked[u][:, a:b]
             nc.vector.tensor_tensor(diff[u][:, a:b], src, y[u][:, a:b], ALU.subtract)
 
-        def gate(u, a=0, b=CH):
+        def gate(u, a=0, b=CH, tag=None):
             if u not in gated:
-                gated[u] = tile_of("gated", u)
+                gated[u] = tile_of("gated", u, tag)
             nc.vector.scalar_tensor_tensor(gated[u][:, a:b], th[u][:, a:b], 1.0, diff[u][:, a:b], ALU.add, ALU.mult)
 
         def finish(u, a=0, b=CH, tag=None):
@@ -172,22 +175,35 @@ def tile_picked_highway_gelu_p_kernel(tc, x_words, x_scales, res, w1, w2, offs, 
         for i, u in ((LAYER, q0), (LAYER, q2), (GATE, q0), (GATE, q2), (LAYER, q1), (GATE, q1), (LAYER, q3), (GATE, q3)):
             product(i, u)
 
+        zero[q2] = keep.tile([P, 1], F32, name="zero", tag="hold")
+        nc.gpsimd.memset(zero[q2][:], 0.0)
         layer(q0)
         layer(q2)
         gate_tanh(q0)
         pick(q1)
         layer(q1)
         gate_tanh(q1)
-        gate_tanh(q2)
+        gate_tanh(q2, hold=q2)
         pick(q2, H, CH)
         pick(q3)
         layer(q3)
         gate_tanh(q3)
 
-        for u in (q0, q1, q2, q3):
+        def halves(step, u, **how):
             for a in (0, H):
-                subtract(u, a, a + H, fused=(u == q0 or (u == q2 and a == 0)))
-            for a in (0, H):
-                gate(u, a, a + H)
-            for a, b in ((0, H), (H, CH)) if u != q3 else ((0, H), (H, CH - P), (CH - P, CH)):
-                finish(u, a, b)
+                step(u, a, a + H, **how)
+
+        halves(subtract, q0, fused=True)
+        halves(gate, q0)
+        halves(finish, q0)
+        subtract(q1)
+        subtract(q2, 0, H, fused=True)
+        gate(q1, tag="hold")
+        subtract(q2, H, CH)
+        finish(q1)
+        halves(gate, q2)
+        halves(finish, q2)
+        halves(subtract, q3)
+        halves(gate, q3)
+        for a, b in ((0, H), (H, CH - P), (CH - P, CH)):
+            finish(q3, a, b)

@@ -109,6 +109,8 @@ def tile_picked_highway_gelu_p_kernel(tc, x_words, x_scales, res, w1, w2, offs, 
             if (kind, u) in on_res:
                 m, slot = on_res[kind, u]
                 return shared.tile([P, CH], F32, name=name, align_bytes=64, offset=res_at[m] + 4 * CH * slot)
+            if (kind, u) in on_zero:
+                return shared.tile([P, CH], F32, name=name, align_bytes=64, offset=on_zero[kind, u])
             return keep.tile([P, CH], F32, name=name, tag=tag or name)
 
         def product(i, u):
@@ -133,14 +135,14 @@ def tile_picked_highway_gelu_p_kernel(tc, x_words, x_scales, res, w1, w2, offs, 
             if hold is None:
                 nc.scalar.activation(y[u][:], acc[LAYER, u][:], ACT.Gelu_apprx_tanh)
             else:
-                nc.scalar.activation(y[u][:], acc[LAYER, u][:], ACT.Gelu_apprx_tanh, bias=zero[hold][:])
+                nc.scalar.activation(y[u][:], acc[LAYER, u][:], ACT.Gelu_apprx_tanh, bias=zero[hold][:, 0:1])
 
         def gate_tanh(u, hold=None):
             th[u] = tile_of("th", u)
             if hold is None:
                 nc.scalar.activation(th[u][:], acc[GATE, u][:], ACT.Tanh, scale=-0.5)
             else:
-                nc.scalar.activation(th[u][:], acc[GATE, u][:], ACT.Tanh, scale=-0.5, bias=zero[hold][:])
+                nc.scalar.activation(th[u][:], acc[GATE, u][:], ACT.Tanh, scale=-0.5, bias=zero[hold][:, 0:1])
 
         def looked_up(u, a, b):
             m, c = u
@@ -170,13 +172,15 @@ def tile_picked_highway_gelu_p_kernel(tc, x_words, x_scales, res, w1, w2, offs, 
             nc.sync.dma_start(out=out[block(m), c * CH + a : c * CH + b], in_=piece[:])
 
         q0, q1, q2, q3 = (0, 0), (0, 1), (1, 0), (1, 1)
-        on_res = {("y", q3): (1, 0), ("th", q3): (1, 1)}
+        on_res = {("th", q3): (1, 1)}
 
         for i, u in ((LAYER, q0), (LAYER, q2), (GATE, q0), (GATE, q2), (LAYER, q1), (GATE, q1), (LAYER, q3), (GATE, q3)):
             product(i, u)
 
-        zero[q2] = keep.tile([P, 1], F32, name="zero", tag="hold")
-        nc.gpsimd.memset(zero[q2][:], 0.0)
+        zero_at = res_at[1] + 4 * T + 4 * CH
+        on_zero = {("gated", q1): zero_at + 64 - 4 * CH, ("y", q3): zero_at + 64}
+        zero[q2] = shared.tile([P, 32], F32, name="zero", align_bytes=64, offset=zero_at)
+        nc.gpsimd.memset(zero[q2][:, 0:1], 0.0)
         layer(q0)
         layer(q2)
         gate_tanh(q0)
@@ -185,8 +189,9 @@ def tile_picked_highway_gelu_p_kernel(tc, x_words, x_scales, res, w1, w2, offs, 
         gate_tanh(q1)
         gate_tanh(q2, hold=q2)
         pick(q2, H, CH)
-        pick(q3)
         layer(q3)
+        pick(q3, 0, H)
+        pick(q3, H, CH)
         gate_tanh(q3)
 
         def halves(step, u, **how):
@@ -198,12 +203,14 @@ def tile_picked_highway_gelu_p_kernel(tc, x_words, x_scales, res, w1, w2, offs, 
         halves(finish, q0)
         subtract(q1)
         subtract(q2, 0, H, fused=True)
-        gate(q1, tag="hold")
+        gate(q1)
         subtract(q2, H, CH)
+        gate(q2, 0, H)
         finish(q1)
-        halves(gate, q2)
-        halves(finish, q2)
+        gate(q2, H, CH)
         halves(subtract, q3)
+        finish(q2, 0, CH - P)
         halves(gate, q3)
+        finish(q2, CH - P, CH)
         for a, b in ((0, H), (H, CH - P), (CH - P, CH)):
             finish(q3, a, b)

@@ -137,8 +137,8 @@ def tile_picked_highway_gelu_p_kernel(tc, x_words, x_scales, res, w1, w2, offs, 
             else:
                 nc.scalar.activation(y[u][:], acc[LAYER, u][:], ACT.Gelu_apprx_tanh, bias=zero[hold][:, 0:1])
 
-        def gate_tanh(u, hold=None):
-            th[u] = tile_of("th", u)
+        def gate_tanh(u, hold=None, tag=None):
+            th[u] = tile_of("th", u, tag)
             if hold is None:
                 nc.scalar.activation(th[u][:], acc[GATE, u][:], ACT.Tanh, scale=-0.5)
             else:
@@ -172,11 +172,12 @@ def tile_picked_highway_gelu_p_kernel(tc, x_words, x_scales, res, w1, w2, offs, 
             nc.sync.dma_start(out=out[block(m), c * CH + a : c * CH + b], in_=piece[:])
 
         q0, q1, q2, q3 = (0, 0), (0, 1), (1, 0), (1, 1)
-        on_res = {("th", q3): (1, 1)}
+        on_res = {}
 
         for i, u in ((LAYER, q0), (LAYER, q2), (GATE, q0), (GATE, q2), (LAYER, q1), (GATE, q1), (LAYER, q3), (GATE, q3)):
             product(i, u)
 
+        FUSED = 320
         zero_at = res_at[1] + 4 * T + 4 * CH
         on_zero = {("gated", q1): zero_at + 64 - 4 * CH, ("y", q3): zero_at + 64}
         zero[q2] = shared.tile([P, 32], F32, name="zero", align_bytes=64, offset=zero_at)
@@ -188,11 +189,10 @@ def tile_picked_highway_gelu_p_kernel(tc, x_words, x_scales, res, w1, w2, offs, 
         layer(q1)
         gate_tanh(q1)
         gate_tanh(q2, hold=q2)
-        pick(q2, H, CH)
+        pick(q2, FUSED, CH)
         layer(q3)
         pick(q3, 0, H)
         pick(q3, H, CH)
-        gate_tanh(q3)
 
         def halves(step, u, **how):
             for a in (0, H):
@@ -202,9 +202,10 @@ def tile_picked_highway_gelu_p_kernel(tc, x_words, x_scales, res, w1, w2, offs, 
         halves(gate, q0)
         halves(finish, q0)
         subtract(q1)
-        subtract(q2, 0, H, fused=True)
+        subtract(q2, 0, FUSED, fused=True)
         gate(q1)
-        subtract(q2, H, CH)
+        subtract(q2, FUSED, CH)
+        gate_tanh(q3, tag="picked10")
         gate(q2, 0, H)
         finish(q1)
         gate(q2, H, CH)

@@ -164,12 +164,15 @@ def tile_picked_highway_gelu_p_kernel(tc, x_words, x_scales, res, w1, w2, offs, 
                 gated[u] = tile_of("gated", u, tag)
             nc.vector.scalar_tensor_tensor(gated[u][:, a:b], th[u][:, a:b], 1.0, diff[u][:, a:b], ALU.add, ALU.mult)
 
-        def finish(u, a=0, b=CH, tag=None):
+        results = {}
+
+        def finish(u, a=0, b=CH, store_from=None):
             m, c = u
-            name = f"result{m}{c}{a}"
-            piece = keep.tile([P, b - a], F32, name=name, tag=tag or name)
-            nc.vector.scalar_tensor_tensor(piece[:], gated[u][:, a:b], 0.5, y[u][:, a:b], ALU.mult, ALU.add)
-            nc.sync.dma_start(out=out[block(m), c * CH + a : c * CH + b], in_=piece[:])
+            if u not in results:
+                results[u] = tile_of("result", u)
+            nc.vector.scalar_tensor_tensor(results[u][:, a:b], gated[u][:, a:b], 0.5, y[u][:, a:b], ALU.mult, ALU.add)
+            if store_from is not None:
+                nc.sync.dma_start(out=out[block(m), c * CH + store_from : c * CH + b], in_=results[u][:, store_from:b])
 
         q0, q1, q2, q3 = (0, 0), (0, 1), (1, 0), (1, 1)
         on_res = {}
@@ -177,7 +180,7 @@ def tile_picked_highway_gelu_p_kernel(tc, x_words, x_scales, res, w1, w2, offs, 
         for i, u in ((LAYER, q0), (LAYER, q2), (GATE, q0), (GATE, q2), (LAYER, q1), (GATE, q1), (LAYER, q3), (GATE, q3)):
             product(i, u)
 
-        FUSED = 320
+        FUSED = 256
         zero_at = res_at[1] + 4 * T + 4 * CH
         on_zero = {("gated", q1): zero_at + 64 - 4 * CH, ("y", q3): zero_at + 64}
         zero[q2] = shared.tile([P, 32], F32, name="zero", align_bytes=64, offset=zero_at)
@@ -200,18 +203,17 @@ def tile_picked_highway_gelu_p_kernel(tc, x_words, x_scales, res, w1, w2, offs, 
 
         halves(subtract, q0, fused=True)
         halves(gate, q0)
-        halves(finish, q0)
+        finish(q0, 0, H)
+        finish(q0, H, CH, store_from=0)
         subtract(q1)
         subtract(q2, 0, FUSED, fused=True)
         gate(q1)
         subtract(q2, FUSED, CH)
         gate_tanh(q3, tag="picked10")
-        gate(q2, 0, H)
-        finish(q1)
-        gate(q2, H, CH)
+        finish(q1, store_from=0)
+        gate(q2)
         halves(subtract, q3)
-        finish(q2, 0, CH - P)
+        finish(q2, store_from=0)
         halves(gate, q3)
-        finish(q2, CH - P, CH)
         for a, b in ((0, H), (H, CH - P), (CH - P, CH)):
-            finish(q3, a, b)
+            finish(q3, a, b, store_from=a)

@@ -1,6 +1,7 @@
 from contextlib import ExitStack
 
 import concourse.mybir as mybir
+from concourse.masks import make_identity
 
 K, T, S, N = 512, 2048, 1024, 256
 FLOPS = 2 * 2 * K * N * S
@@ -54,6 +55,9 @@ def tile_picked_highway_gelu_p_kernel(tc, x_words, x_scales, res, w1, w2, offs, 
                 in_=x_scales[0, SCALE_ROWS * q : SCALE_ROWS * (q + 1), :].bitcast(I32),
             )
 
+        identity = keep.tile([P, P], F32, name="identity")
+        make_identity(nc, identity[:])
+
         RAW_BYTES = PACK * N * 4
         raw_at = {GATE: 0, LAYER: RAW_BYTES}
         raw = {}
@@ -99,8 +103,7 @@ def tile_picked_highway_gelu_p_kernel(tc, x_words, x_scales, res, w1, w2, offs, 
         gather(words1[1][:], word_table, CH + H, S)
         quantize(GATE)
         bytes1 = shared.tile([P, CH], U8, name="bytes1", align_bytes=64, offset=raw_at[GATE])
-        for a in (0, H):
-            gather(bytes1[:, a : a + H], scale_table, CH + a, CH + a + H)
+        gather(bytes1[:], scale_table, CH, S)
 
         acc, y, th, picked, diff, gated, zero = {}, {}, {}, {}, {}, {}, {}
 
@@ -115,7 +118,7 @@ def tile_picked_highway_gelu_p_kernel(tc, x_words, x_scales, res, w1, w2, offs, 
 
         def product(i, u):
             m, c = u
-            acc[i, u] = psum.tile([P, CH], F32, name=f"acc{i}{m}{c}")
+            acc[i, u] = psum.tile([P, CH], F32, name=f"acc{i}{m}{c}", tag=f"acc{i}{m}{c}")
             pieces = [(0, CH, words0[:], bytes0[:])]
             if c == 1:
                 pieces = [(a, a + H, words1[a // H][:], bytes1[:, a : a + H]) for a in (0, H)]
@@ -130,8 +133,8 @@ def tile_picked_highway_gelu_p_kernel(tc, x_words, x_scales, res, w1, w2, offs, 
                     stop=True,
                 )
 
-        def layer(u, hold=None):
-            y[u] = tile_of("y", u)
+        def layer(u, hold=None, tag=None):
+            y[u] = tile_of("y", u, tag)
             if hold is None:
                 nc.scalar.activation(y[u][:], acc[LAYER, u][:], ACT.Gelu_apprx_tanh)
             else:
@@ -142,16 +145,16 @@ def tile_picked_highway_gelu_p_kernel(tc, x_words, x_scales, res, w1, w2, offs, 
             if hold is None:
                 nc.scalar.activation(th[u][:], acc[GATE, u][:], ACT.Tanh, scale=-0.5)
             else:
-                nc.scalar.activation(th[u][:], acc[GATE, u][:], ACT.Tanh, scale=-0.5, bias=zero[hold][:, 0:1])
+                nc.scalar.activation(th[u][:], acc[GATE, u][:], ACT.Tanh, scale=zero[hold][:, 0:1])
 
         def looked_up(u, a, b):
             m, c = u
             return res_rows[m][:].indirect(entries(c * CH + a, c * CH + b))
 
-        def pick(u, a=0, b=CH):
+        def pick(u, a=0, b=CH, scale=1.0):
             if u not in picked:
                 picked[u] = tile_of("picked", u)
-            nc.scalar.activation(picked[u][:, a:b], looked_up(u, a, b), ACT.Copy)
+            nc.scalar.activation(picked[u][:, a:b], looked_up(u, a, b), ACT.Copy, scale=scale)
 
         def subtract(u, a=0, b=CH, fused=False):
             if u not in diff:
@@ -177,43 +180,74 @@ def tile_picked_highway_gelu_p_kernel(tc, x_words, x_scales, res, w1, w2, offs, 
         q0, q1, q2, q3 = (0, 0), (0, 1), (1, 0), (1, 1)
         on_res = {}
 
-        for i, u in ((LAYER, q0), (LAYER, q2), (GATE, q0), (GATE, q2), (LAYER, q1), (GATE, q1), (LAYER, q3), (GATE, q3)):
+        for i, u in ((LAYER, q0), (LAYER, q2), (GATE, q0), (GATE, q2), (LAYER, q1)):
             product(i, u)
+        acc[GATE, q1] = psum.tile([P, CH], F32, name="acc101")
+        for n in range(CH // P):
+            a = n * P
+            nc.tensor.matmul_mx(
+                out=acc[GATE, q1][:, block(n)],
+                lhsT=words1[a // H][:, a % H : a % H + P].bitcast(FP4X4),
+                lhsT_scale=bytes1[:, block(n)],
+                rhs=codes[GATE, 0][:].bitcast(FP8X4),
+                rhs_scale=scales[GATE, 0][:],
+                start=True,
+                stop=True,
+            )
+        for i in (LAYER, GATE):
+            product(i, q3)
 
-        FUSED = 256
+        def add_turned(dst, sources):
+            steps = [(n, src) for src in sources for n in range(CH // P)]
+            for k, (n, src) in enumerate(steps):
+                nc.tensor.matmul(
+                    dst[:, block(n)],
+                    src[:, block(n)],
+                    identity[:],
+                    start=(k == 0),
+                    stop=(k == len(steps) - 1),
+                    is_transpose=True,
+                )
+
         zero_at = res_at[1] + 4 * T + 4 * CH
         on_zero = {("gated", q1): zero_at + 64 - 4 * CH, ("y", q3): zero_at + 64}
         zero[q2] = shared.tile([P, 32], F32, name="zero", align_bytes=64, offset=zero_at)
-        nc.gpsimd.memset(zero[q2][:, 0:1], 0.0)
+        nc.gpsimd.memset(zero[q2][:, 0:1], -0.5)
         layer(q0)
         layer(q2)
         gate_tanh(q0)
-        pick(q1)
+        pick(q1, scale=-1.0)
         layer(q1)
         gate_tanh(q1)
         gate_tanh(q2, hold=q2)
-        pick(q2, FUSED, CH)
-        layer(q3)
         pick(q3, 0, H)
+        layer(q3)
         pick(q3, H, CH)
 
         def halves(step, u, **how):
             for a in (0, H):
                 step(u, a, a + H, **how)
 
+        turned_diff = psum.tile([P, CH], F32, name="turned_diff", tag="acc000")
+        add_turned(turned_diff, [picked[q1], y[q1]])
+
         halves(subtract, q0, fused=True)
         halves(gate, q0)
         finish(q0, 0, H)
         finish(q0, H, CH, store_from=0)
-        subtract(q1)
-        subtract(q2, 0, FUSED, fused=True)
-        gate(q1)
-        subtract(q2, FUSED, CH)
-        gate_tanh(q3, tag="picked10")
-        finish(q1, store_from=0)
+        subtract(q2, fused=True)
+        gated[q1] = tile_of("gated", q1)
+        nc.vector.scalar_tensor_tensor(gated[q1][:], th[q1][:], 1.0, turned_diff[:], ALU.add, ALU.mult)
+        back = psum.tile([P, CH], F32, name="back", tag="acc010")
+        add_turned(back, [gated[q1]])
         gate(q2)
-        halves(subtract, q3)
+        gate_tanh(q3, tag="diff10")
+        subtract(q3, 0, H)
         finish(q2, store_from=0)
+        subtract(q3, H, CH)
+        second = tile_of("result", q1)
+        nc.vector.scalar_tensor_tensor(second[:], back[:], -0.5, y[q1][:], ALU.mult, ALU.add)
+        nc.sync.dma_start(out=out[block(0), CH:S], in_=second[:])
         halves(gate, q3)
         for a, b in ((0, H), (H, CH - P), (CH - P, CH)):
             finish(q3, a, b, store_from=a)

from contextlib import ExitStack

import concourse.mybir as mybir
from concourse.masks import make_identity

K, T, S, N = 512, 2048, 1024, 256
FLOPS = 2 * 2 * K * N * S

F32 = mybir.dt.float32
BF16 = mybir.dt.bfloat16
I32 = mybir.dt.int32
U32 = mybir.dt.uint32
U16 = mybir.dt.uint16
U8 = mybir.dt.uint8
FP8X4 = mybir.dt.float8_e4m3fn_x4
FP4X4 = mybir.dt.float4_e2m1fn_x4
ACT = mybir.ActivationFunctionType
ALU = mybir.AluOpType

P = 128
PACK = 4
RUN = 4
QUADRANT = 32
SCALE_ROWS = 4
PER_COL = 16
CH = 512
H = CH // 2
LAYER, GATE = 0, 1


def tile_picked_highway_gelu_p_kernel(tc, x_words, x_scales, res, w1, w2, offs, out):
    nc = tc.nc
    with ExitStack() as ctx:
        keep = ctx.enter_context(tc.tile_pool(name="keep", bufs=1))
        shared = ctx.enter_context(tc.tile_pool(name="shared", bufs=1))
        psum = ctx.enter_context(tc.psum_pool(name="psum", bufs=1))

        def block(b):
            return slice(b * P, (b + 1) * P)

        word_table = keep.tile([P, T], U16, name="word_table", align_bytes=64)
        nc.sync.dma_start(out=word_table[:].bitcast(I32), in_=x_words[0].bitcast(I32))
        offsets = keep.tile([P, S // PER_COL], U16, name="offsets")
        nc.sync.dma_start(offsets[:], offs)

        scale_table = keep.tile([P, T], U8, name="scale_table", align_bytes=64)
        nc.gpsimd.memset(scale_table[:].bitcast(I32), 0)
        warm_in = keep.tile([P, 1], F32, name="warm_in")
        warm_out = keep.tile([P, 1], F32, name="warm_out")
        nc.gpsimd.memset(warm_in[:], 0.0)
        nc.scalar.activation(warm_out[:], warm_in[:], ACT.Gelu_apprx_tanh)
        for q in range(P // QUADRANT):
            nc.sync.dma_start(
                out=scale_table[QUADRANT * q : QUADRANT * q + SCALE_ROWS, :].bitcast(I32),
                in_=x_scales[0, SCALE_ROWS * q : SCALE_ROWS * (q + 1), :].bitcast(I32),
            )

        identity = keep.tile([P, P], F32, name="identity")
        make_identity(nc, identity[:])

        RAW_BYTES = PACK * N * 4
        raw_at = {GATE: 0, LAYER: RAW_BYTES}
        raw = {}
        for i, w in ((LAYER, w1), (GATE, w2)):
            raw[i] = shared.tile([P, PACK, N], F32, name=f"raw{i}", align_bytes=64, offset=raw_at[i])
            nc.sync.dma_start(out=raw[i][:], in_=w.rearrange("(p t) c -> p t c", t=PACK))
        res_at = [2 * RAW_BYTES, 2 * RAW_BYTES + 4 * T]
        res_rows = []
        for m in range(N // P):
            rows = shared.tile([P, T], F32, name=f"res_rows{m}", align_bytes=64, offset=res_at[m])
            nc.sync.dma_start(out=rows[:], in_=res[block(m), :])
            res_rows.append(rows)

        grouped, codes, scales = {}, {}, {}
        for i in (LAYER, GATE):
            for m in range(N // P):
                grouped[i, m] = keep.tile([P, P * PACK], BF16, name=f"grouped{i}{m}", align_bytes=64)
                codes[i, m] = keep.tile([P, P], U32, name=f"codes{i}{m}", align_bytes=64)
                scales[i, m] = keep.tile([P, P], U8, name=f"scales{i}{m}", align_bytes=64)
                nc.scalar.copy(
                    out=grouped[i, m][:].rearrange("p (c r t) -> p c t r", r=RUN, t=PACK),
                    in_=raw[i][:, :, block(m)].rearrange("p t (c r) -> p c t r", r=RUN),
                )

        def quantize(i):
            for m in range(N // P):
                nc.vector.quantize_mx(out=codes[i, m][:].bitcast(FP8X4), scales=scales[i, m][:], in_=grouped[i, m][:])

        def entries(a, b):
            return offsets[:, a // PER_COL : b // PER_COL]

        def gather(dst, table, a, b):
            nc.vector.tensor_copy(dst, table[:].indirect(entries(a, b)))

        words0 = keep.tile([P, CH], U16, name="words0", align_bytes=64)
        gather(words0[:], word_table, 0, CH)
        bytes0 = keep.tile([P, CH], U8, name="bytes0", align_bytes=64)
        gather(bytes0[:], scale_table, 0, CH)
        words1 = [keep.tile([P, H], U16, name="words1a", align_bytes=64)]
        gather(words1[0][:], word_table, CH, CH + H)
        quantize(LAYER)
        words1.append(shared.tile([P, H], U16, name="words1b", align_bytes=64, offset=raw_at[LAYER]))
        gather(words1[1][:], word_table, CH + H, S)
        quantize(GATE)
        bytes1 = shared.tile([P, CH], U8, name="bytes1", align_bytes=64, offset=raw_at[GATE])
        gather(bytes1[:], scale_table, CH, S)

        acc, y, th, picked, diff, gated, zero = {}, {}, {}, {}, {}, {}, {}

        def tile_of(kind, u, tag=None):
            name = f"{kind}{u[0]}{u[1]}"
            if (kind, u) in on_res:
                m, slot = on_res[kind, u]
                return shared.tile([P, CH], F32, name=name, align_bytes=64, offset=res_at[m] + 4 * CH * slot)
            if (kind, u) in on_zero:
                return shared.tile([P, CH], F32, name=name, align_bytes=64, offset=on_zero[kind, u])
            return keep.tile([P, CH], F32, name=name, tag=tag or name)

        def product(i, u):
            m, c = u
            acc[i, u] = psum.tile([P, CH], F32, name=f"acc{i}{m}{c}", tag=f"acc{i}{m}{c}")
            pieces = [(0, CH, words0[:], bytes0[:])]
            if c == 1:
                pieces = [(a, a + H, words1[a // H][:], bytes1[:, a : a + H]) for a in (0, H)]
            for a, b, words, scale_bytes in pieces:
                nc.tensor.matmul_mx(
                    out=acc[i, u][:, a:b],
                    lhsT=codes[i, m][:].bitcast(FP8X4),
                    lhsT_scale=scales[i, m][:],
                    rhs=words.bitcast(FP4X4),
                    rhs_scale=scale_bytes,
                    start=True,
                    stop=True,
                )

        def layer(u, hold=None, tag=None):
            y[u] = tile_of("y", u, tag)
            if hold is None:
                nc.scalar.activation(y[u][:], acc[LAYER, u][:], ACT.Gelu_apprx_tanh)
            else:
                nc.scalar.activation(y[u][:], acc[LAYER, u][:], ACT.Gelu_apprx_tanh, bias=zero[hold][:, 0:1])

        def gate_tanh(u, hold=None, tag=None):
            th[u] = tile_of("th", u, tag)
            if hold is None:
                nc.scalar.activation(th[u][:], acc[GATE, u][:], ACT.Tanh, scale=-0.5)
            else:
                nc.scalar.activation(th[u][:], acc[GATE, u][:], ACT.Tanh, scale=zero[hold][:, 0:1])

        def looked_up(u, a, b):
            m, c = u
            return res_rows[m][:].indirect(entries(c * CH + a, c * CH + b))

        def pick(u, a=0, b=CH, scale=1.0):
            if u not in picked:
                picked[u] = tile_of("picked", u)
            nc.scalar.activation(picked[u][:, a:b], looked_up(u, a, b), ACT.Copy, scale=scale)

        def subtract(u, a=0, b=CH, fused=False):
            if u not in diff:
                diff[u] = tile_of("diff", u)
            src = looked_up(u, a, b) if fused else picked[u][:, a:b]
            nc.vector.tensor_tensor(diff[u][:, a:b], src, y[u][:, a:b], ALU.subtract)

        def gate(u, a=0, b=CH, tag=None):
            if u not in gated:
                gated[u] = tile_of("gated", u, tag)
            nc.vector.scalar_tensor_tensor(gated[u][:, a:b], th[u][:, a:b], 1.0, diff[u][:, a:b], ALU.add, ALU.mult)

        results = {}

        def finish(u, a=0, b=CH, store_from=None):
            m, c = u
            if u not in results:
                results[u] = tile_of("result", u)
            nc.vector.scalar_tensor_tensor(results[u][:, a:b], gated[u][:, a:b], 0.5, y[u][:, a:b], ALU.mult, ALU.add)
            if store_from is not None:
                nc.sync.dma_start(out=out[block(m), c * CH + store_from : c * CH + b], in_=results[u][:, store_from:b])

        q0, q1, q2, q3 = (0, 0), (0, 1), (1, 0), (1, 1)
        on_res = {}

        for i, u in ((LAYER, q0), (LAYER, q2), (GATE, q0), (GATE, q2), (LAYER, q1)):
            product(i, u)
        acc[GATE, q1] = psum.tile([P, CH], F32, name="acc101")
        for n in range(CH // P):
            a = n * P
            nc.tensor.matmul_mx(
                out=acc[GATE, q1][:, block(n)],
                lhsT=words1[a // H][:, a % H : a % H + P].bitcast(FP4X4),
                lhsT_scale=bytes1[:, block(n)],
                rhs=codes[GATE, 0][:].bitcast(FP8X4),
                rhs_scale=scales[GATE, 0][:],
                start=True,
                stop=True,
            )
        for i in (LAYER, GATE):
            product(i, q3)

        def add_turned(dst, sources):
            steps = [(n, src) for src in sources for n in range(CH // P)]
            for k, (n, src) in enumerate(steps):
                nc.tensor.matmul(
                    dst[:, block(n)],
                    src[:, block(n)],
                    identity[:],
                    start=(k == 0),
                    stop=(k == len(steps) - 1),
                    is_transpose=True,
                )

        zero_at = res_at[1] + 4 * T + 4 * CH
        on_zero = {("gated", q1): zero_at + 64 - 4 * CH, ("y", q3): zero_at + 64}
        zero[q2] = shared.tile([P, 32], F32, name="zero", align_bytes=64, offset=zero_at)
        nc.gpsimd.memset(zero[q2][:, 0:1], -0.5)
        layer(q0)
        layer(q2)
        gate_tanh(q0)
        pick(q1, scale=-1.0)
        layer(q1)
        gate_tanh(q1)
        gate_tanh(q2, hold=q2)
        pick(q3, 0, H)
        layer(q3)
        pick(q3, H, CH)

        def halves(step, u, **how):
            for a in (0, H):
                step(u, a, a + H, **how)

        turned_diff = psum.tile([P, CH], F32, name="turned_diff", tag="acc000")
        add_turned(turned_diff, [picked[q1], y[q1]])

        halves(subtract, q0, fused=True)
        halves(gate, q0)
        finish(q0, 0, H)
        finish(q0, H, CH, store_from=0)
        subtract(q2, fused=True)
        gated[q1] = tile_of("gated", q1)
        nc.vector.scalar_tensor_tensor(gated[q1][:], th[q1][:], 1.0, turned_diff[:], ALU.add, ALU.mult)
        back = psum.tile([P, CH], F32, name="back", tag="acc010")
        add_turned(back, [gated[q1]])
        gate(q2)
        gate_tanh(q3, tag="diff10")
        subtract(q3, 0, H)
        finish(q2, store_from=0)
        subtract(q3, H, CH)
        second = tile_of("result", q1)
        nc.vector.scalar_tensor_tensor(second[:], back[:], -0.5, y[q1][:], ALU.mult, ALU.add)
        nc.sync.dma_start(out=out[block(0), CH:S], in_=second[:])
        halves(gate, q3)
        for a, b in ((0, H), (H, CH - P), (CH - P, CH)):
            finish(q3, a, b, store_from=a)
